import numpy as np
import ml_dtypes


def mxq(x, axis, fmt="e4m3"):
    dtype, down = {"e4m3": (ml_dtypes.float8_e4m3fn, 7), "e5m2": (ml_dtypes.float8_e5m2, 14)}[fmt]
    v = np.moveaxis(np.asarray(x, np.float32).astype(ml_dtypes.bfloat16).astype(np.float64), axis, -1)
    blocks = v.reshape(v.shape[:-1] + (-1, 32))
    amax = np.abs(blocks).max(-1, keepdims=True)
    byte = np.maximum(np.where(amax > 0, np.frexp(amax)[1] - 1 + 127, 0) - down, 1)
    scale = np.exp2(byte - 127.0)
    codes = (blocks / scale).astype(np.float32).astype(dtype).astype(np.float64)
    return np.moveaxis((codes * scale).reshape(v.shape), -1, axis)


WIDE = False


def mx_kscale(k):
    if not WIDE:
        return np.ones(k)
    levels = np.array([10, -10, 5, -5, 0])
    if k % 512:
        return np.exp2(np.random.permutation(np.resize(levels, k // 32))).repeat(32)
    a = np.empty((k // 512, 16))
    for p in range(k // 512):
        a[p, :8] = np.random.permutation(np.resize(levels, 8))
        for g in range(8):
            far = levels[np.abs(levels - a[p, g]) >= 10]
            a[p, g + 8] = far[np.random.randint(len(far))]
    return np.exp2(a.ravel()).repeat(32)


def f64(x):
    return np.asarray(x).astype(np.float64)


def striped(idx):
    return np.tile(idx.reshape(-1, 16).T, (8, 1)).astype(np.uint16)


def unstriped(offs):
    return offs[:16].T.reshape(-1).astype(np.int64)


def striped8(idx):
    return np.concatenate([x.reshape(-1, 16).T for x in idx]).astype(np.uint16)


def runs(offs, k):
    lists = np.stack([offs[16 * r : 16 * r + 16].T.reshape(-1) for r in range(8)]).astype(np.int64)
    return lists[np.arange(k) % 512 // 64]


def pack_weight(w):
    k, n = w.shape
    w = f64(np.asarray(w, np.float32).astype(ml_dtypes.bfloat16)).reshape(k // 32, 32, n)
    amax = np.abs(w).max(1)
    byte = np.clip(np.where(amax > 0, np.frexp(amax)[1] - 1 + 127 - 7, 1), 1, 254)
    scaled = (w * np.exp2(127.0 - byte)[:, None, :]).reshape(k, n).astype(np.float32)
    words = np.ascontiguousarray(scaled.reshape(k // 512, 128, 4, n).transpose(0, 1, 3, 2)).astype(ml_dtypes.float8_e4m3fn).view(np.uint8)
    return words, np.ascontiguousarray(byte.astype(np.uint8).reshape(k // 512, 16, n))


def unpack_weight(words, scales):
    g, p, n, _ = words.shape
    vals = np.ascontiguousarray(words).view(ml_dtypes.float8_e4m3fn).astype(np.float64) * np.repeat(np.exp2(scales.astype(np.float64) - 127.0), 8, axis=1)[..., None]
    return vals.transpose(0, 1, 3, 2).reshape(g * 512, n)


K, T, S, N, H = 512, 2048, 512, 512, 512


def setup_inputs():
    n = np.random.standard_normal
    s = mx_kscale(K)[:, None]
    u = mx_kscale(H)
    packed_xT = pack_weight(n((K, T)) * s)
    return {
        "x_words": packed_xT[0],
        "x_scales": packed_xT[1],
        "w1": (n((K, H)) / np.sqrt(K) / s * u).astype(np.float32),
        "w2": (n((K, H)) / np.sqrt(K) / s).astype(np.float32),
        "w3": (n((H, N)) / np.sqrt(2 * H) / u[:, None]).astype(np.float32),
        "w4": (n((H, N)) / np.sqrt(2 * H) / u[:, None]).astype(np.float32),
        "offs": striped(np.random.permutation(T)[:S]),
        "p1": striped8(np.stack([np.random.permutation(S) for _ in range(8)])),
        "p2": striped8(np.stack([np.random.permutation(S) for _ in range(8)])),
    }


def reference(x_words, x_scales, w1, w2, w3, w4, offs, p1, p2):
    xq = unpack_weight(x_words, x_scales)[:, unstriped(offs)]
    y = mxq(f64(w1), 0, "e4m3").T @ xq
    h1 = y[np.arange(H)[:, None], runs(p1, H)]
    h2 = y[np.arange(H)[:, None], runs(p2, H)]
    z = y + h1 + h2
    c = mxq(f64(w2), 0, "e4m3").T @ xq
    z2 = c * h1 + c * h2
    return mxq(f64(w3), 0, "e4m3").T @ mxq(z, 0, "e4m3") + mxq(f64(w4), 0, "e4m3").T @ mxq(z2, 0, "e4m3")

@@ -1,0 +1,139 @@
+from contextlib import ExitStack
+
+import concourse.mybir as mybir
+
+K, T, S, N, H = 512, 2048, 512, 512, 512
+FLOPS = 4 * 2 * 512 * 512 * 512
+
+F32 = mybir.dt.float32
+BF16 = mybir.dt.bfloat16
+I32 = mybir.dt.int32
+U32 = mybir.dt.uint32
+U16 = mybir.dt.uint16
+U8 = mybir.dt.uint8
+FP8X4 = mybir.dt.float8_e4m3fn_x4
+ADD = mybir.AluOpType.add
+MULT = mybir.AluOpType.mult
+
+P = 128
+PACK = 4
+SUB = 128
+HALF = 256
+BLOCKS = [(0, 256), (256, 128), (384, 128)]
+
+
+def tile_picked_ngcf8_none_p_kernel(tc, x_words, x_scales, w1, w2, w3, w4, offs, p1, p2, out):
+    nc = tc.nc
+    with ExitStack() as ctx:
+        keep = ctx.enter_context(tc.tile_pool(name="keep", bufs=1))
+        ring = ctx.enter_context(tc.tile_pool(name="ring", bufs=2))
+        psum_wide = ctx.enter_context(tc.psum_pool(name="psum_wide", bufs=4))
+        psum_sub = ctx.enter_context(tc.psum_pool(name="psum_sub", bufs=2))
+
+        offs_sb = keep.tile([P, S // 16], U16, name="offs_sb")
+        p1_sb = keep.tile([P, S // 16], U16, name="p1_sb")
+        p2_sb = keep.tile([P, S // 16], U16, name="p2_sb")
+        xw_all = keep.tile([P, T], I32, name="xw_all", align_bytes=64)
+        xs_all = keep.tile([P, T], U8, name="xs_all", align_bytes=64)
+        xw = keep.tile([P, S], U32, name="xw", align_bytes=64)
+        xs = keep.tile([P, S], U8, name="xs", align_bytes=64)
+
+        def rows(w):
+            return w.rearrange("(p j) c -> p j c", j=PACK)
+
+        nc.vector.memset(xs_all[:].bitcast(I32), 0)
+        nc.sync.dma_start(offs_sb[:], offs)
+        for q in range(4):
+            nc.scalar.dma_start(out=xs_all[32 * q : 32 * q + 4, :].bitcast(I32), in_=x_scales[0][4 * q : 4 * q + 4, :].bitcast(I32))
+        w1_raw = [keep.tile([P, PACK, HALF], F32, name=f"w1_raw{h}") for h in range(2)]
+        for h in range(2):
+            nc.sync.dma_start(out=w1_raw[h][:], in_=rows(w1)[:, :, h * HALF : (h + 1) * HALF])
+        nc.sync.dma_start(out=xw_all[:], in_=x_words[0].rearrange("p n t -> p (n t)").bitcast(I32))
+        nc.sync.dma_start(p1_sb[:], p1)
+        nc.sync.dma_start(p2_sb[:], p2)
+        w_raw = {}
+        for name, w in (("w2", w2), ("w3", w3), ("w4", w4)):
+            w_raw[name] = keep.tile([P, PACK, H], F32, name=f"{name}_raw")
+            nc.sync.dma_start(out=w_raw[name][:], in_=rows(w))
+
+        w_bf = {n: keep.tile([P, PACK * H], BF16, name=f"{n}_bf", align_bytes=64) for n in ("w1", "w2", "w3", "w4")}
+        w_codes = {n: keep.tile([P, H], U32, name=f"{n}_codes", align_bytes=64) for n in ("w1", "w2", "w3", "w4")}
+        w_scale = {n: keep.tile([P, H], U8, name=f"{n}_scale", align_bytes=64) for n in ("w1", "w2", "w3", "w4")}
+
+        def dealt_out(n):
+            return w_bf[n][:].rearrange("p (t m j) -> p m j t", t=PACK, j=PACK)
+
+        def dealt_in(raw):
+            return raw[:].rearrange("p j (m t) -> p m j t", t=PACK)
+
+        def quantize_w(n):
+            nc.vector.quantize_mx(out=w_codes[n][:].bitcast(FP8X4), scales=w_scale[n][:], in_=w_bf[n][:])
+
+        def mm(dst, n, tile_index, codes, scales, start, stop):
+            cols = slice(tile_index * P, (tile_index + 1) * P)
+            nc.tensor.matmul_mx(out=dst, lhsT=w_codes[n][:, cols].bitcast(FP8X4), lhsT_scale=w_scale[n][:, cols],
+                                rhs=codes.bitcast(FP8X4), rhs_scale=scales, start=start, stop=stop)
+
+        nc.vector.tensor_copy(xs[:], xs_all[:].indirect(offs_sb[:]))
+        m_half = P // 2
+        nc.scalar.copy(out=dealt_out("w1")[:, 0:m_half], in_=dealt_in(w1_raw[0]))
+        nc.vector.tensor_copy(out=dealt_out("w1")[:, m_half:P], in_=dealt_in(w1_raw[1]))
+        quantize_w("w1")
+
+        y_win = [keep.tile([P, S], F32, name=f"y_win{t}") for t in range(PACK)]
+        for h in range(2):
+            nc.vector.tensor_copy(xw[:, h * HALF : (h + 1) * HALF], xw_all[:].bitcast(U32).indirect(offs_sb[:, h * 16 : (h + 1) * 16]))
+        for t in range(PACK):
+            for h in range(2):
+                cols = slice(h * HALF, (h + 1) * HALF)
+                acc = psum_wide.tile([P, HALF], F32, name="wide")
+                mm(acc[:], "w1", t, xw[:, cols], xs[:, cols], True, True)
+                nc.scalar.copy(out=y_win[t][:, cols], in_=acc[:])
+
+        nc.scalar.copy(out=dealt_out("w2"), in_=dealt_in(w_raw["w2"]))
+        for n in ("w3", "w4"):
+            nc.scalar.copy(out=w_bf[n][:].rearrange("p (c i j) -> p c j i", i=4, j=PACK),
+                           in_=w_raw[n][:].rearrange("p j (c i) -> p c j i", i=4))
+
+        out_rows = out.rearrange("(a p) j -> p a j", p=P)
+        for b, (j0, width) in enumerate(BLOCKS):
+            lists = slice(j0 // 16, (j0 + width) // 16)
+            h1 = ring.tile([P, PACK, width], F32, name="h1")
+            hs = ring.tile([P, PACK, width], F32, name="hs")
+            for t in range(PACK):
+                nc.vector.tensor_copy(h1[:, t, :], y_win[t][:].indirect(p1_sb[:, lists]))
+            for t in range(PACK):
+                nc.vector.tensor_tensor(hs[:, t, :], y_win[t][:].indirect(p2_sb[:, lists]), h1[:, t, :], ADD)
+            if b == 0:
+                quantize_w("w2")
+            z_bf = ring.tile([P, 2, width * PACK], BF16, name="z_bf", align_bytes=64)
+            for n, plane, op in (("w1", 0, ADD), ("w2", 1, MULT)):
+                for u in range(width // SUB):
+                    cols = slice(j0 + u * SUB, j0 + (u + 1) * SUB)
+                    own = psum_sub.tile([P, PACK, SUB], F32, name=f"own_{n}")
+                    for t in range(PACK):
+                        mm(own[:, t, :], n, t, xw[:, cols], xs[:, cols], True, True)
+                    nc.vector.tensor_tensor(
+                        z_bf[:, plane, u * SUB * PACK : (u + 1) * SUB * PACK].rearrange("p (c i t) -> p c t i", i=4, t=PACK),
+                        own[:].rearrange("p t (c i) -> p c t i", i=4),
+                        hs[:, :, u * SUB : (u + 1) * SUB].rearrange("p t (c i) -> p c t i", i=4),
+                        op,
+                    )
+            if b == 0:
+                quantize_w("w3")
+                quantize_w("w4")
+            z_codes = ring.tile([P, 2, width], U32, name="z_codes", align_bytes=64)
+            z_scale = ring.tile([P, 2, width], U8, name="z_scale", align_bytes=64)
+            for plane in range(2):
+                nc.vector.quantize_mx(out=z_codes[:, plane, :].bitcast(FP8X4), scales=z_scale[:, plane, :], in_=z_bf[:, plane, :])
+            res = ring.tile([P, PACK, width], F32, name="res")
+            accs = [psum_wide.tile([P, width], F32, name="wide") for a in range(PACK)]
+            for plane, n in enumerate(("w3", "w4")):
+                for a in range(PACK):
+                    mm(accs[a][:], n, a, z_codes[:, plane, :], z_scale[:, plane, :], plane == 0, plane == 1)
+            for a in range(PACK):
+                if b == len(BLOCKS) - 1 and a % 2 == 1:
+                    nc.vector.tensor_copy(out=res[:, a, :], in_=accs[a][:])
+                else:
+                    nc.scalar.copy(out=res[:, a, :], in_=accs[a][:])
+            nc.sync.dma_start(out=out_rows[:, :, j0 : j0 + width], in_=res[:])

@@ -1,6 +1,7 @@
 from contextlib import ExitStack
 
 import concourse.mybir as mybir
+from concourse.masks import make_identity
 
 K, T, S, N, H = 512, 2048, 512, 512, 512
 FLOPS = 4 * 2 * 512 * 512 * 512
@@ -26,9 +27,10 @@ def tile_picked_ngcf8_none_p_kernel(tc, x_words, x_scales, w1, w2, w3, w4, offs,
     nc = tc.nc
     with ExitStack() as ctx:
         keep = ctx.enter_context(tc.tile_pool(name="keep", bufs=1))
-        ring = ctx.enter_context(tc.tile_pool(name="ring", bufs=2))
-        psum_wide = ctx.enter_context(tc.psum_pool(name="psum_wide", bufs=4))
-        psum_sub = ctx.enter_context(tc.psum_pool(name="psum_sub", bufs=2))
+        psum = ctx.enter_context(tc.psum_pool(name="psum", bufs=1))
+
+        def bank(index, shape):
+            return psum.tile(shape, F32, name=f"bank{index}")
 
         offs_sb = keep.tile([P, S // 16], U16, name="offs_sb")
         p1_sb = keep.tile([P, S // 16], U16, name="p1_sb")
@@ -41,13 +43,13 @@ def tile_picked_ngcf8_none_p_kernel(tc, x_words, x_scales, w1, w2, w3, w4, offs,
         def rows(w):
             return w.rearrange("(p j) c -> p j c", j=PACK)
 
-        nc.vector.memset(xs_all[:].bitcast(I32), 0)
-        nc.sync.dma_start(offs_sb[:], offs)
-        for q in range(4):
-            nc.scalar.dma_start(out=xs_all[32 * q : 32 * q + 4, :].bitcast(I32), in_=x_scales[0][4 * q : 4 * q + 4, :].bitcast(I32))
+        nc.gpsimd.memset(xs_all[:].bitcast(I32), 0)
         w1_raw = [keep.tile([P, PACK, HALF], F32, name=f"w1_raw{h}") for h in range(2)]
-        for h in range(2):
-            nc.sync.dma_start(out=w1_raw[h][:], in_=rows(w1)[:, :, h * HALF : (h + 1) * HALF])
+        nc.sync.dma_start(out=w1_raw[0][:], in_=rows(w1)[:, :, 0:HALF])
+        for q in range(4):
+            nc.sync.dma_start(out=xs_all[32 * q : 32 * q + 4, :].bitcast(I32), in_=x_scales[0][4 * q : 4 * q + 4, :].bitcast(I32))
+        nc.sync.dma_start(offs_sb[:], offs)
+        nc.sync.dma_start(out=w1_raw[1][:], in_=rows(w1)[:, :, HALF:H])
         nc.sync.dma_start(out=xw_all[:], in_=x_words[0].rearrange("p n t -> p (n t)").bitcast(I32))
         nc.sync.dma_start(p1_sb[:], p1)
         nc.sync.dma_start(p2_sb[:], p2)
@@ -56,15 +58,16 @@ def tile_picked_ngcf8_none_p_kernel(tc, x_words, x_scales, w1, w2, w3, w4, offs,
             w_raw[name] = keep.tile([P, PACK, H], F32, name=f"{name}_raw")
             nc.sync.dma_start(out=w_raw[name][:], in_=rows(w))
 
+        ident = keep.tile([P, P], F32, name="ident")
+        make_identity(nc, ident[:])
         w_bf = {n: keep.tile([P, PACK * H], BF16, name=f"{n}_bf", align_bytes=64) for n in ("w1", "w2", "w3", "w4")}
         w_codes = {n: keep.tile([P, H], U32, name=f"{n}_codes", align_bytes=64) for n in ("w1", "w2", "w3", "w4")}
         w_scale = {n: keep.tile([P, H], U8, name=f"{n}_scale", align_bytes=64) for n in ("w1", "w2", "w3", "w4")}
 
-        def dealt_out(n):
-            return w_bf[n][:].rearrange("p (t m j) -> p m j t", t=PACK, j=PACK)
-
-        def dealt_in(raw):
-            return raw[:].rearrange("p j (m t) -> p m j t", t=PACK)
+        def cast_dealt(copy, n, raw, m_range):
+            for h in range(2):
+                copy(out=w_bf[n][:].rearrange("p (h e m j) -> p h m j e", h=2, e=2, j=PACK)[:, h, m_range],
+                     in_=raw[:].rearrange("p j (m h e) -> p h m j e", h=2, e=2)[:, h])
 
         def quantize_w(n):
             nc.vector.quantize_mx(out=w_codes[n][:].bitcast(FP8X4), scales=w_scale[n][:], in_=w_bf[n][:])
@@ -76,64 +79,127 @@ def tile_picked_ngcf8_none_p_kernel(tc, x_words, x_scales, w1, w2, w3, w4, offs,
 
         nc.vector.tensor_copy(xs[:], xs_all[:].indirect(offs_sb[:]))
         m_half = P // 2
-        nc.scalar.copy(out=dealt_out("w1")[:, 0:m_half], in_=dealt_in(w1_raw[0]))
-        nc.vector.tensor_copy(out=dealt_out("w1")[:, m_half:P], in_=dealt_in(w1_raw[1]))
+        cast_dealt(nc.scalar.copy, "w1", w1_raw[0], slice(0, m_half))
+        cast_dealt(nc.vector.tensor_copy, "w1", w1_raw[1], slice(m_half, P))
         quantize_w("w1")
 
         y_win = [keep.tile([P, S], F32, name=f"y_win{t}") for t in range(PACK)]
         for h in range(2):
             nc.vector.tensor_copy(xw[:, h * HALF : (h + 1) * HALF], xw_all[:].bitcast(U32).indirect(offs_sb[:, h * 16 : (h + 1) * 16]))
-        for t in range(PACK):
-            for h in range(2):
-                cols = slice(h * HALF, (h + 1) * HALF)
-                acc = psum_wide.tile([P, HALF], F32, name="wide")
-                mm(acc[:], "w1", t, xw[:, cols], xs[:, cols], True, True)
-                nc.scalar.copy(out=y_win[t][:, cols], in_=acc[:])
+        pieces = [(0, 0, HALF), (0, HALF, HALF)] + [(t, 0, S) for t in range(1, PACK)]
+        for index, (t, j0, width) in enumerate(pieces):
+            cols = slice(j0, j0 + width)
+            acc = bank(index % 4, [P, width])
+            mm(acc[:], "w1", t, xw[:, cols], xs[:, cols], True, True)
+            nc.scalar.copy(out=y_win[t][:, cols], in_=acc[:])
 
-        nc.scalar.copy(out=dealt_out("w2"), in_=dealt_in(w_raw["w2"]))
+        cast_dealt(nc.scalar.copy, "w2", w_raw["w2"], slice(0, P))
         for n in ("w3", "w4"):
-            nc.scalar.copy(out=w_bf[n][:].rearrange("p (c i j) -> p c j i", i=4, j=PACK),
-                           in_=w_raw[n][:].rearrange("p j (c i) -> p c j i", i=4))
+            nc.scalar.copy(out=w_bf[n][:].rearrange("p (c i j) -> p c j i", i=2, j=PACK),
+                           in_=w_raw[n][:].rearrange("p j (c i) -> p c j i", i=2))
 
+        zt_all = keep.tile([P, (S - SUB) * PACK], BF16, name="w4_raw")
+        turned = [bank(4 + v, [P, PACK, SUB]) for v in range(3)]
+        for v in range(3):
+            for t in range(PACK):
+                nc.tensor.matmul(turned[v][:, t, :], lhsT=y_win[t][:, v * SUB : (v + 1) * SUB], rhs=ident[:], is_transpose=True, start=t == 0, stop=False)
         out_rows = out.rearrange("(a p) j -> p a j", p=P)
-        for b, (j0, width) in enumerate(BLOCKS):
-            lists = slice(j0 // 16, (j0 + width) // 16)
-            h1 = ring.tile([P, PACK, width], F32, name="h1")
-            hs = ring.tile([P, PACK, width], F32, name="hs")
-            for t in range(PACK):
-                nc.vector.tensor_copy(h1[:, t, :], y_win[t][:].indirect(p1_sb[:, lists]))
-            for t in range(PACK):
-                nc.vector.tensor_tensor(hs[:, t, :], y_win[t][:].indirect(p2_sb[:, lists]), h1[:, t, :], ADD)
+        first_tags = ([f"h1_0_{t}" for t in range(PACK - 1)] + ["w2_bf"], "h1_1", "z_bf0")
+        sum_tags = ("hs_0", "w2_bf", "z_bf1")
+        h1, hs, z_bf = {}, {}, {}
+
+        def fetch_first(b):
+            j0, width = BLOCKS[b]
             if b == 0:
-                quantize_w("w2")
-            z_bf = ring.tile([P, 2, width * PACK], BF16, name="z_bf", align_bytes=64)
-            for n, plane, op in (("w1", 0, ADD), ("w2", 1, MULT)):
-                for u in range(width // SUB):
-                    cols = slice(j0 + u * SUB, j0 + (u + 1) * SUB)
-                    own = psum_sub.tile([P, PACK, SUB], F32, name=f"own_{n}")
-                    for t in range(PACK):
-                        mm(own[:, t, :], n, t, xw[:, cols], xs[:, cols], True, True)
-                    nc.vector.tensor_tensor(
-                        z_bf[:, plane, u * SUB * PACK : (u + 1) * SUB * PACK].rearrange("p (c i t) -> p c t i", i=4, t=PACK),
-                        own[:].rearrange("p t (c i) -> p c t i", i=4),
-                        hs[:, :, u * SUB : (u + 1) * SUB].rearrange("p t (c i) -> p c t i", i=4),
-                        op,
-                    )
-            if b == 0:
-                quantize_w("w3")
-                quantize_w("w4")
-            z_codes = ring.tile([P, 2, width], U32, name="z_codes", align_bytes=64)
-            z_scale = ring.tile([P, 2, width], U8, name="z_scale", align_bytes=64)
-            for plane in range(2):
-                nc.vector.quantize_mx(out=z_codes[:, plane, :].bitcast(FP8X4), scales=z_scale[:, plane, :], in_=z_bf[:, plane, :])
-            res = ring.tile([P, PACK, width], F32, name="res")
-            accs = [psum_wide.tile([P, width], F32, name="wide") for a in range(PACK)]
-            for plane, n in enumerate(("w3", "w4")):
+                h1[b] = [keep.tile([P, width], F32, name=first_tags[b][t], align_bytes=64)[:] for t in range(PACK)]
+            else:
+                whole = keep.tile([P, PACK, width], F32, name=first_tags[b], align_bytes=64)
+                h1[b] = [whole[:, t, :] for t in range(PACK)]
+            for t in range(PACK):
+                nc.vector.tensor_copy(h1[b][t], y_win[t][:].indirect(p1_sb[:, j0 // 16 : (j0 + width) // 16]))
+
+        def fetch_second(b):
+            j0, width = BLOCKS[b]
+            hs[b] = keep.tile([P, PACK, width], F32, name=sum_tags[b], align_bytes=64)
+            for t in range(PACK):
+                nc.vector.tensor_tensor(hs[b][:, t, :], y_win[t][:].indirect(p2_sb[:, j0 // 16 : (j0 + width) // 16]), h1[b][t], ADD)
+
+        def with_own(b, n, plane, op, u, own):
+            j0, width = BLOCKS[b]
+            cols = slice(j0 + u * SUB, j0 + (u + 1) * SUB)
+            for t in range(PACK):
+                mm(own[:, t, :], n, t, xw[:, cols], xs[:, cols], True, True)
+            nc.vector.tensor_tensor(
+                z_bf[b][:, (plane * width + u * SUB) * PACK : (plane * width + (u + 1) * SUB) * PACK].rearrange("p (c i t) -> p c t i", i=2, t=PACK),
+                own[:].rearrange("p t (c i) -> p c t i", i=2),
+                hs[b][:, :, u * SUB : (u + 1) * SUB].rearrange("p t (c i) -> p c t i", i=2),
+                op,
+            )
+
+        def sum_turned(b):
+            j0, width = BLOCKS[b]
+            subs = width // SUB
+            back = bank(7 if b == 0 else 5, [P, subs, 2, SUB])
+            for u in range(subs):
+                v = j0 // SUB + u
+                for t in range(PACK):
+                    nc.tensor.matmul(turned[v][:, t, :], lhsT=hs[b][:, t, u * SUB : (u + 1) * SUB], rhs=ident[:], is_transpose=True, start=False, stop=t == PACK - 1)
+                zt_bf = zt_all[:, v * SUB * PACK : (v + 1) * SUB * PACK]
+                nc.scalar.copy(out=zt_bf.rearrange("k (h p e) -> k h p e", h=2, e=2), in_=turned[v][:].rearrange("k (h e) p -> k h p e", e=2))
+                for h in range(2):
+                    nc.tensor.transpose(back[:, u, h, :], zt_bf.bitcast(F32)[:, h * P : (h + 1) * P], ident[:])
+            nc.scalar.copy(out=z_bf[b][:, 0 : width * PACK].bitcast(F32).rearrange("p (u k h) -> p u k h", u=subs, h=2),
+                           in_=back[:].rearrange("p u h k -> p u k h"))
+
+        def finish(b):
+            j0, width = BLOCKS[b]
+            z_codes = keep.tile([P, 2, width], U32, name=f"z_codes{b}", align_bytes=64)
+            z_scale = keep.tile([P, 2, width], U8, name=f"z_scale{b}", align_bytes=64)
+            res = keep.tile([P, PACK, width], F32, name=f"res{b}")
+            if b == 2:
+                for plane in range(2):
+                    nc.vector.quantize_mx(out=z_codes[:, plane, :].bitcast(FP8X4), scales=z_scale[:, plane, :], in_=z_bf[b][:, plane * width * PACK : (plane + 1) * width * PACK])
+                accs = [bank((5 + a) % 8, [P, width]) for a in range(PACK)]
+                for plane, n in enumerate(("w3", "w4")):
+                    for a in range(PACK):
+                        mm(accs[a][:], n, a, z_codes[:, plane, :], z_scale[:, plane, :], plane == 0, plane == 1)
                 for a in range(PACK):
-                    mm(accs[a][:], n, a, z_codes[:, plane, :], z_scale[:, plane, :], plane == 0, plane == 1)
-            for a in range(PACK):
-                if b == len(BLOCKS) - 1 and a % 2 == 1:
-                    nc.vector.tensor_copy(out=res[:, a, :], in_=accs[a][:])
-                else:
-                    nc.scalar.copy(out=res[:, a, :], in_=accs[a][:])
-            nc.sync.dma_start(out=out_rows[:, :, j0 : j0 + width], in_=res[:])
+                    if a % 2 == 1:
+                        nc.vector.tensor_copy(out=res[:, a, :], in_=accs[a][:])
+                    else:
+                        nc.scalar.copy(out=res[:, a, :], in_=accs[a][:])
+                nc.sync.dma_start(out=out_rows[:, 0:2, j0 : j0 + width], in_=res[:, 0:2, :])
+                nc.scalar.dma_start(out=out_rows[:, 2:4, j0 : j0 + width], in_=res[:, 2:4, :])
+            else:
+                nc.vector.quantize_mx(out=z_codes[:].rearrange("p a n -> p (a n)").bitcast(FP8X4), scales=z_scale[:].rearrange("p a n -> p (a n)"),
+                                      in_=z_bf[b][:])
+                per_bank = S // width
+                for g in range(PACK // per_bank):
+                    acc = bank(j0 // SUB + g, [P, per_bank, width])
+                    for a in range(per_bank):
+                        for plane, n in enumerate(("w3", "w4")):
+                            mm(acc[:, a, :], n, g * per_bank + a, z_codes[:, plane, :], z_scale[:, plane, :], plane == 0, plane == 1)
+                    rows_g = slice(g * per_bank, (g + 1) * per_bank)
+                    nc.scalar.copy(out=res[:, rows_g, :], in_=acc[:])
+                    nc.sync.dma_start(out=out_rows[:, rows_g, j0 : j0 + width], in_=res[:, rows_g, :])
+
+        quantize_w("w2")
+        for b in range(3):
+            z_bf[b] = keep.tile([P, 2 * BLOCKS[b][1] * PACK], BF16, name=f"z_bf{b}", align_bytes=64)
+        for b in range(2):
+            fetch_first(b)
+            fetch_second(b)
+        for b in range(2):
+            sum_turned(b)
+        for b in range(2):
+            for u in range(BLOCKS[b][1] // SUB):
+                with_own(b, "w2", 1, MULT, u, bank(BLOCKS[b][0] // SUB + u, [P, PACK, SUB]))
+        quantize_w("w3")
+        quantize_w("w4")
+        finish(0)
+        finish(1)
+        fetch_first(2)
+        fetch_second(2)
+        with_own(2, "w1", 0, ADD, 0, bank(4, [P, PACK, SUB]))
+        with_own(2, "w2", 1, MULT, 0, bank(3, [P, PACK, SUB]))
+        finish(2)

@@ -3,7 +3,7 @@ from contextlib import ExitStack
 import concourse.mybir as mybir
 from concourse.masks import make_identity
 
-K, T, S, N, H = 512, 2048, 512, 512, 512
+T, S, H = 2048, 512, 512
 FLOPS = 4 * 2 * 512 * 512 * 512
 
 F32 = mybir.dt.float32
@@ -19,8 +19,16 @@ MULT = mybir.AluOpType.mult
 P = 128
 PACK = 4
 SUB = 128
-HALF = 256
-BLOCKS = [(0, 256), (256, 128), (384, 128)]
+HALF = S // 2
+BLOCKS = [(0, HALF), (HALF, SUB), (HALF + SUB, SUB)]
+LAST = len(BLOCKS) - 1
+TURNED = (S - SUB) // SUB
+
+Y_BANKS = 4
+TURN_BANK = 4
+BACK_BANKS = (7, 5)
+LAST_Y_BANK, LAST_C_BANK = 4, 6
+LAST_OUT_BANKS = (5, 3, 7, 0)
 
 
 def tile_picked_ngcf8_none_p_kernel(tc, x_words, x_scales, w1, w2, w3, w4, offs, p1, p2, out):
@@ -32,6 +40,12 @@ def tile_picked_ngcf8_none_p_kernel(tc, x_words, x_scales, w1, w2, w3, w4, offs,
         def bank(index, shape):
             return psum.tile(shape, F32, name=f"bank{index}")
 
+        def list_columns(j0, width):
+            return slice(j0 // 16, (j0 + width) // 16)
+
+        def rows(w):
+            return w.rearrange("(p j) c -> p j c", j=PACK)
+
         offs_sb = keep.tile([P, S // 16], U16, name="offs_sb")
         p1_sb = keep.tile([P, S // 16], U16, name="p1_sb")
         p2_sb = keep.tile([P, S // 16], U16, name="p2_sb")
@@ -40,16 +54,13 @@ def tile_picked_ngcf8_none_p_kernel(tc, x_words, x_scales, w1, w2, w3, w4, offs,
         xw = keep.tile([P, S], U32, name="xw", align_bytes=64)
         xs = keep.tile([P, S], U8, name="xs", align_bytes=64)
 
-        def rows(w):
-            return w.rearrange("(p j) c -> p j c", j=PACK)
-
         nc.gpsimd.memset(xs_all[:].bitcast(I32), 0)
-        w1_raw = [keep.tile([P, PACK, HALF], F32, name=f"w1_raw{h}") for h in range(2)]
-        nc.sync.dma_start(out=w1_raw[0][:], in_=rows(w1)[:, :, 0:HALF])
+        w1_raw = keep.tile([P, PACK, H], F32, name="w1_raw")
+        nc.sync.dma_start(out=w1_raw[:, 0:2, :], in_=rows(w1)[:, 0:2, :])
         for q in range(4):
             nc.sync.dma_start(out=xs_all[32 * q : 32 * q + 4, :].bitcast(I32), in_=x_scales[0][4 * q : 4 * q + 4, :].bitcast(I32))
         nc.sync.dma_start(offs_sb[:], offs)
-        nc.sync.dma_start(out=w1_raw[1][:], in_=rows(w1)[:, :, HALF:H])
+        nc.sync.dma_start(out=w1_raw[:, 2:4, :], in_=rows(w1)[:, 2:4, :])
         nc.sync.dma_start(out=xw_all[:], in_=x_words[0].rearrange("p n t -> p (n t)").bitcast(I32))
         nc.sync.dma_start(p1_sb[:], p1)
         nc.sync.dma_start(p2_sb[:], p2)
@@ -60,14 +71,15 @@ def tile_picked_ngcf8_none_p_kernel(tc, x_words, x_scales, w1, w2, w3, w4, offs,
 
         ident = keep.tile([P, P], F32, name="ident")
         make_identity(nc, ident[:])
-        w_bf = {n: keep.tile([P, PACK * H], BF16, name=f"{n}_bf", align_bytes=64) for n in ("w1", "w2", "w3", "w4")}
-        w_codes = {n: keep.tile([P, H], U32, name=f"{n}_codes", align_bytes=64) for n in ("w1", "w2", "w3", "w4")}
-        w_scale = {n: keep.tile([P, H], U8, name=f"{n}_scale", align_bytes=64) for n in ("w1", "w2", "w3", "w4")}
+        names = ("w1", "w2", "w3", "w4")
+        w_bf = {n: keep.tile([P, PACK * H], BF16, name=f"{n}_bf", align_bytes=64) for n in names}
+        w_codes = {n: keep.tile([P, H], U32, name=f"{n}_codes", align_bytes=64) for n in names}
+        w_scale = {n: keep.tile([P, H], U8, name=f"{n}_scale", align_bytes=64) for n in names}
 
-        def cast_dealt(copy, n, raw, m_range):
-            for h in range(2):
-                copy(out=w_bf[n][:].rearrange("p (h e m j) -> p h m j e", h=2, e=2, j=PACK)[:, h, m_range],
-                     in_=raw[:].rearrange("p j (m h e) -> p h m j e", h=2, e=2)[:, h])
+        def cast_dealt(copy, n, raw, h):
+            half = w_bf[n][:, h * 2 * H : (h + 1) * 2 * H]
+            copy(out=half.rearrange("p (e m j) -> p m j e", e=2, j=PACK),
+                 in_=raw[:].rearrange("p j (m h e) -> p h m j e", h=2, e=2)[:, h])
 
         def quantize_w(n):
             nc.vector.quantize_mx(out=w_codes[n][:].bitcast(FP8X4), scales=w_scale[n][:], in_=w_bf[n][:])
@@ -78,59 +90,59 @@ def tile_picked_ngcf8_none_p_kernel(tc, x_words, x_scales, w1, w2, w3, w4, offs,
                                 rhs=codes.bitcast(FP8X4), rhs_scale=scales, start=start, stop=stop)
 
         nc.vector.tensor_copy(xs[:], xs_all[:].indirect(offs_sb[:]))
-        m_half = P // 2
-        cast_dealt(nc.scalar.copy, "w1", w1_raw[0], slice(0, m_half))
-        cast_dealt(nc.vector.tensor_copy, "w1", w1_raw[1], slice(m_half, P))
-        quantize_w("w1")
+        for h in range(2):
+            cast_dealt(nc.vector.tensor_copy, "w1", w1_raw, h)
+        for h in range(2):
+            cols = slice(h * HALF, (h + 1) * HALF)
+            nc.vector.quantize_mx(out=w_codes["w1"][:, cols].bitcast(FP8X4), scales=w_scale["w1"][:, cols], in_=w_bf["w1"][:, h * 2 * H : (h + 1) * 2 * H])
+        for h in range(2):
+            nc.vector.tensor_copy(xw[:, h * HALF : (h + 1) * HALF], xw_all[:].bitcast(U32).indirect(offs_sb[:, list_columns(h * HALF, HALF)]))
 
         y_win = [keep.tile([P, S], F32, name=f"y_win{t}") for t in range(PACK)]
-        for h in range(2):
-            nc.vector.tensor_copy(xw[:, h * HALF : (h + 1) * HALF], xw_all[:].bitcast(U32).indirect(offs_sb[:, h * 16 : (h + 1) * 16]))
         pieces = [(0, 0, HALF), (0, HALF, HALF)] + [(t, 0, S) for t in range(1, PACK)]
         for index, (t, j0, width) in enumerate(pieces):
             cols = slice(j0, j0 + width)
-            acc = bank(index % 4, [P, width])
+            acc = bank(index % Y_BANKS, [P, width])
             mm(acc[:], "w1", t, xw[:, cols], xs[:, cols], True, True)
             nc.scalar.copy(out=y_win[t][:, cols], in_=acc[:])
 
-        cast_dealt(nc.scalar.copy, "w2", w_raw["w2"], slice(0, P))
+        for h in range(2):
+            cast_dealt(nc.scalar.copy, "w2", w_raw["w2"], h)
         for n in ("w3", "w4"):
             nc.scalar.copy(out=w_bf[n][:].rearrange("p (c i j) -> p c j i", i=2, j=PACK),
                            in_=w_raw[n][:].rearrange("p j (c i) -> p c j i", i=2))
 
-        zt_all = keep.tile([P, (S - SUB) * PACK], BF16, name="w4_raw")
-        turned = [bank(4 + v, [P, PACK, SUB]) for v in range(3)]
-        for v in range(3):
+        zt_all = keep.tile([P, TURNED * SUB * PACK], BF16, name="w4_raw")
+        turned = [bank(TURN_BANK + v, [P, PACK, SUB]) for v in range(TURNED)]
+        for v in range(TURNED):
             for t in range(PACK):
                 nc.tensor.matmul(turned[v][:, t, :], lhsT=y_win[t][:, v * SUB : (v + 1) * SUB], rhs=ident[:], is_transpose=True, start=t == 0, stop=False)
+
         out_rows = out.rearrange("(a p) j -> p a j", p=P)
-        first_tags = ([f"h1_0_{t}" for t in range(PACK - 1)] + ["w2_bf"], "h1_1", "z_bf0")
-        sum_tags = ("hs_0", "w2_bf", "z_bf1")
+        first_tags = ("h1_0", "h1_1", "w2_raw")
+        sum_tags = ("hs_0", "hs_1", "z_bf0")
         h1, hs, z_bf = {}, {}, {}
 
         def fetch_first(b):
             j0, width = BLOCKS[b]
-            if b == 0:
-                h1[b] = [keep.tile([P, width], F32, name=first_tags[b][t], align_bytes=64)[:] for t in range(PACK)]
-            else:
-                whole = keep.tile([P, PACK, width], F32, name=first_tags[b], align_bytes=64)
-                h1[b] = [whole[:, t, :] for t in range(PACK)]
+            h1[b] = keep.tile([P, PACK, width], F32, name=first_tags[b])
             for t in range(PACK):
-                nc.vector.tensor_copy(h1[b][t], y_win[t][:].indirect(p1_sb[:, j0 // 16 : (j0 + width) // 16]))
+                nc.vector.tensor_copy(h1[b][:, t, :], y_win[t][:].indirect(p1_sb[:, list_columns(j0, width)]))
 
         def fetch_second(b):
             j0, width = BLOCKS[b]
             hs[b] = keep.tile([P, PACK, width], F32, name=sum_tags[b], align_bytes=64)
             for t in range(PACK):
-                nc.vector.tensor_tensor(hs[b][:, t, :], y_win[t][:].indirect(p2_sb[:, j0 // 16 : (j0 + width) // 16]), h1[b][t], ADD)
+                nc.vector.tensor_tensor(hs[b][:, t, :], y_win[t][:].indirect(p2_sb[:, list_columns(j0, width)]), h1[b][:, t, :], ADD)
 
-        def with_own(b, n, plane, op, u, own):
+        def with_own(b, n, which, op, u, own):
             j0, width = BLOCKS[b]
             cols = slice(j0 + u * SUB, j0 + (u + 1) * SUB)
             for t in range(PACK):
                 mm(own[:, t, :], n, t, xw[:, cols], xs[:, cols], True, True)
+            first = (which * width + u * SUB) * PACK
             nc.vector.tensor_tensor(
-                z_bf[b][:, (plane * width + u * SUB) * PACK : (plane * width + (u + 1) * SUB) * PACK].rearrange("p (c i t) -> p c t i", i=2, t=PACK),
+                z_bf[b][:, first : first + SUB * PACK].rearrange("p (c i t) -> p c t i", i=2, t=PACK),
                 own[:].rearrange("p t (c i) -> p c t i", i=2),
                 hs[b][:, :, u * SUB : (u + 1) * SUB].rearrange("p t (c i) -> p c t i", i=2),
                 op,
@@ -139,7 +151,7 @@ def tile_picked_ngcf8_none_p_kernel(tc, x_words, x_scales, w1, w2, w3, w4, offs,
         def sum_turned(b):
             j0, width = BLOCKS[b]
             subs = width // SUB
-            back = bank(7 if b == 0 else 5, [P, subs, 2, SUB])
+            back = bank(BACK_BANKS[b], [P, subs, 2, SUB])
             for u in range(subs):
                 v = j0 // SUB + u
                 for t in range(PACK):
@@ -156,50 +168,51 @@ def tile_picked_ngcf8_none_p_kernel(tc, x_words, x_scales, w1, w2, w3, w4, offs,
             z_codes = keep.tile([P, 2, width], U32, name=f"z_codes{b}", align_bytes=64)
             z_scale = keep.tile([P, 2, width], U8, name=f"z_scale{b}", align_bytes=64)
             res = keep.tile([P, PACK, width], F32, name=f"res{b}")
-            if b == 2:
-                for plane in range(2):
-                    nc.vector.quantize_mx(out=z_codes[:, plane, :].bitcast(FP8X4), scales=z_scale[:, plane, :], in_=z_bf[b][:, plane * width * PACK : (plane + 1) * width * PACK])
-                accs = [bank((5 + a) % 8, [P, width]) for a in range(PACK)]
-                for plane, n in enumerate(("w3", "w4")):
+            if b == LAST:
+                for which in range(2):
+                    nc.vector.quantize_mx(out=z_codes[:, which, :].bitcast(FP8X4), scales=z_scale[:, which, :],
+                                          in_=z_bf[b][:, which * width * PACK : (which + 1) * width * PACK])
+                accs = [bank(index, [P, width]) for index in LAST_OUT_BANKS]
+                for which, n in enumerate(("w3", "w4")):
                     for a in range(PACK):
-                        mm(accs[a][:], n, a, z_codes[:, plane, :], z_scale[:, plane, :], plane == 0, plane == 1)
+                        mm(accs[a][:], n, a, z_codes[:, which, :], z_scale[:, which, :], which == 0, which == 1)
                 for a in range(PACK):
-                    if a % 2 == 1:
-                        nc.vector.tensor_copy(out=res[:, a, :], in_=accs[a][:])
-                    else:
-                        nc.scalar.copy(out=res[:, a, :], in_=accs[a][:])
+                    copy = nc.vector.tensor_copy if a % 2 == 1 else nc.scalar.copy
+                    copy(out=res[:, a, :], in_=accs[a][:])
                 nc.sync.dma_start(out=out_rows[:, 0:2, j0 : j0 + width], in_=res[:, 0:2, :])
                 nc.scalar.dma_start(out=out_rows[:, 2:4, j0 : j0 + width], in_=res[:, 2:4, :])
             else:
-                nc.vector.quantize_mx(out=z_codes[:].rearrange("p a n -> p (a n)").bitcast(FP8X4), scales=z_scale[:].rearrange("p a n -> p (a n)"),
-                                      in_=z_bf[b][:])
+                nc.vector.quantize_mx(out=z_codes[:].rearrange("p a n -> p (a n)").bitcast(FP8X4),
+                                      scales=z_scale[:].rearrange("p a n -> p (a n)"), in_=z_bf[b][:])
                 per_bank = S // width
                 for g in range(PACK // per_bank):
                     acc = bank(j0 // SUB + g, [P, per_bank, width])
                     for a in range(per_bank):
-                        for plane, n in enumerate(("w3", "w4")):
-                            mm(acc[:, a, :], n, g * per_bank + a, z_codes[:, plane, :], z_scale[:, plane, :], plane == 0, plane == 1)
+                        for which, n in enumerate(("w3", "w4")):
+                            mm(acc[:, a, :], n, g * per_bank + a, z_codes[:, which, :], z_scale[:, which, :], which == 0, which == 1)
                     rows_g = slice(g * per_bank, (g + 1) * per_bank)
                     nc.scalar.copy(out=res[:, rows_g, :], in_=acc[:])
                     nc.sync.dma_start(out=out_rows[:, rows_g, j0 : j0 + width], in_=res[:, rows_g, :])
 
-        quantize_w("w2")
-        for b in range(3):
-            z_bf[b] = keep.tile([P, 2 * BLOCKS[b][1] * PACK], BF16, name=f"z_bf{b}", align_bytes=64)
-        for b in range(2):
+        for b, (j0, width) in enumerate(BLOCKS):
+            z_bf[b] = keep.tile([P, 2 * width * PACK], BF16, name=f"z_bf{b}", align_bytes=64)
+        for b in range(LAST):
             fetch_first(b)
+        for b in range(LAST):
             fetch_second(b)
-        for b in range(2):
+        quantize_w("w2")
+        fetch_first(LAST)
+        for b in range(LAST):
             sum_turned(b)
-        for b in range(2):
-            for u in range(BLOCKS[b][1] // SUB):
-                with_own(b, "w2", 1, MULT, u, bank(BLOCKS[b][0] // SUB + u, [P, PACK, SUB]))
+        for b in range(LAST):
+            j0, width = BLOCKS[b]
+            for u in range(width // SUB):
+                with_own(b, "w2", 1, MULT, u, bank(j0 // SUB + u, [P, PACK, SUB]))
         quantize_w("w3")
         quantize_w("w4")
-        finish(0)
-        finish(1)
-        fetch_first(2)
-        fetch_second(2)
-        with_own(2, "w1", 0, ADD, 0, bank(4, [P, PACK, SUB]))
-        with_own(2, "w2", 1, MULT, 0, bank(3, [P, PACK, SUB]))
-        finish(2)
+        for b in range(LAST):
+            finish(b)
+        fetch_second(LAST)
+        with_own(LAST, "w1", 0, ADD, 0, bank(LAST_Y_BANK, [P, PACK, SUB]))
+        with_own(LAST, "w2", 1, MULT, 0, bank(LAST_C_BANK, [P, PACK, SUB]))
+        finish(LAST)

@@ -20,15 +20,15 @@ P = 128
 PACK = 4
 SUB = 128
 HALF = S // 2
-BLOCKS = [(0, HALF), (HALF, SUB), (HALF + SUB, SUB)]
-LAST = len(BLOCKS) - 1
-TURNED = (S - SUB) // SUB
+RUNS = S // SUB
+SHARE = 84
+WINDOW = 2 * S
 
 Y_BANKS = 4
-TURN_BANK = 4
-BACK_BANKS = (7, 5)
-LAST_Y_BANK, LAST_C_BANK = 4, 6
-LAST_OUT_BANKS = (5, 3, 7, 0)
+TURN_BANKS = ((4, 5), (6, 7))
+C_BANKS = (0, 1, 4, 3)
+BACK_BANKS = (4, 5)
+OUT_BANKS = ((0, 1), (6,), (7, 2, 5, 4))
 
 
 def tile_picked_ngcf8_none_p_kernel(tc, x_words, x_scales, w1, w2, w3, w4, offs, p1, p2, out):
@@ -55,18 +55,18 @@ def tile_picked_ngcf8_none_p_kernel(tc, x_words, x_scales, w1, w2, w3, w4, offs,
         xs = keep.tile([P, S], U8, name="xs", align_bytes=64)
 
         nc.gpsimd.memset(xs_all[:].bitcast(I32), 0)
-        w1_raw = keep.tile([P, PACK, H], F32, name="w1_raw")
-        nc.sync.dma_start(out=w1_raw[:, 0:2, :], in_=rows(w1)[:, 0:2, :])
-        for q in range(4):
-            nc.sync.dma_start(out=xs_all[32 * q : 32 * q + 4, :].bitcast(I32), in_=x_scales[0][4 * q : 4 * q + 4, :].bitcast(I32))
         nc.sync.dma_start(offs_sb[:], offs)
-        nc.sync.dma_start(out=w1_raw[:, 2:4, :], in_=rows(w1)[:, 2:4, :])
         nc.sync.dma_start(out=xw_all[:], in_=x_words[0].rearrange("p n t -> p (n t)").bitcast(I32))
+        for r in range(4):
+            nc.sync.dma_start(out=xs_all[r:P:32, :].bitcast(I32), in_=x_scales[0][r:16:4, :].bitcast(I32))
+        w1_raw = keep.tile([P, PACK, H], F32, name="w1_raw")
+        nc.sync.dma_start(out=w1_raw[:], in_=rows(w1))
         nc.sync.dma_start(p1_sb[:], p1)
-        nc.sync.dma_start(p2_sb[:], p2)
         w_raw = {}
         for name, w in (("w2", w2), ("w3", w3), ("w4", w4)):
-            w_raw[name] = keep.tile([P, PACK, H], F32, name=f"{name}_raw")
+            w_raw[name] = keep.tile([P, PACK, H], F32, name=f"{name}_raw", align_bytes=64)
+            if name == "w4":
+                nc.sync.dma_start(p2_sb[:], p2)
             nc.sync.dma_start(out=w_raw[name][:], in_=rows(w))
 
         ident = keep.tile([P, P], F32, name="ident")
@@ -76,10 +76,10 @@ def tile_picked_ngcf8_none_p_kernel(tc, x_words, x_scales, w1, w2, w3, w4, offs,
         w_codes = {n: keep.tile([P, H], U32, name=f"{n}_codes", align_bytes=64) for n in names}
         w_scale = {n: keep.tile([P, H], U8, name=f"{n}_scale", align_bytes=64) for n in names}
 
-        def cast_dealt(copy, n, raw, h):
+        def cast_dealt(copy, n, raw, h, m0=0, m1=P):
             half = w_bf[n][:, h * 2 * H : (h + 1) * 2 * H]
-            copy(out=half.rearrange("p (e m j) -> p m j e", e=2, j=PACK),
-                 in_=raw[:].rearrange("p j (m h e) -> p h m j e", h=2, e=2)[:, h])
+            copy(out=half.rearrange("p (e m j) -> p m j e", e=2, j=PACK)[:, m0:m1],
+                 in_=raw[:].rearrange("p j (m h e) -> p h m j e", h=2, e=2)[:, h, m0:m1])
 
         def quantize_w(n):
             nc.vector.quantize_mx(out=w_codes[n][:].bitcast(FP8X4), scales=w_scale[n][:], in_=w_bf[n][:])
@@ -89,16 +89,21 @@ def tile_picked_ngcf8_none_p_kernel(tc, x_words, x_scales, w1, w2, w3, w4, offs,
             nc.tensor.matmul_mx(out=dst, lhsT=w_codes[n][:, cols].bitcast(FP8X4), lhsT_scale=w_scale[n][:, cols],
                                 rhs=codes.bitcast(FP8X4), rhs_scale=scales, start=start, stop=stop)
 
+        nc.vector.tensor_copy(xw[:], xw_all[:].bitcast(U32).indirect(offs_sb[:]))
         nc.vector.tensor_copy(xs[:], xs_all[:].indirect(offs_sb[:]))
-        for h in range(2):
-            cast_dealt(nc.vector.tensor_copy, "w1", w1_raw, h)
-        for h in range(2):
-            cols = slice(h * HALF, (h + 1) * HALF)
-            nc.vector.quantize_mx(out=w_codes["w1"][:, cols].bitcast(FP8X4), scales=w_scale["w1"][:, cols], in_=w_bf["w1"][:, h * 2 * H : (h + 1) * 2 * H])
-        for h in range(2):
-            nc.vector.tensor_copy(xw[:, h * HALF : (h + 1) * HALF], xw_all[:].bitcast(U32).indirect(offs_sb[:, list_columns(h * HALF, HALF)]))
 
-        y_win = [keep.tile([P, S], F32, name=f"y_win{t}") for t in range(PACK)]
+        def quantize_w1(c0, c1):
+            nc.vector.quantize_mx(out=w_codes["w1"][:, c0:c1].bitcast(FP8X4), scales=w_scale["w1"][:, c0:c1], in_=w_bf["w1"][:, PACK * c0 : PACK * c1])
+
+        cast_dealt(nc.vector.tensor_copy, "w1", w1_raw, 0, 0, SHARE)
+        cast_dealt(nc.scalar.copy, "w1", w1_raw, 0, SHARE, P)
+        quantize_w1(0, P)
+        quantize_w1(P, 2 * P)
+        cast_dealt(nc.vector.tensor_copy, "w1", w1_raw, 1, 0, SHARE)
+        cast_dealt(nc.scalar.copy, "w1", w1_raw, 1, SHARE, P)
+        quantize_w1(2 * P, 4 * P)
+
+        y_win = [keep.tile([P, WINDOW], F32, name=f"y_win{t}") for t in range(PACK)]
         pieces = [(0, 0, HALF), (0, HALF, HALF)] + [(t, 0, S) for t in range(1, PACK)]
         for index, (t, j0, width) in enumerate(pieces):
             cols = slice(j0, j0 + width)
@@ -112,107 +117,105 @@ def tile_picked_ngcf8_none_p_kernel(tc, x_words, x_scales, w1, w2, w3, w4, offs,
             nc.scalar.copy(out=w_bf[n][:].rearrange("p (c i j) -> p c j i", i=2, j=PACK),
                            in_=w_raw[n][:].rearrange("p j (c i) -> p c j i", i=2))
 
-        zt_all = keep.tile([P, TURNED * SUB * PACK], BF16, name="w4_raw")
-        turned = [bank(TURN_BANK + v, [P, PACK, SUB]) for v in range(TURNED)]
-        for v in range(TURNED):
-            for t in range(PACK):
-                nc.tensor.matmul(turned[v][:, t, :], lhsT=y_win[t][:, v * SUB : (v + 1) * SUB], rhs=ident[:], is_transpose=True, start=t == 0, stop=False)
+        turned = [[bank(TURN_BANKS[h][b], [P, 2, 2, SUB]) for b in range(2)] for h in range(2)]
 
+        def turn(src, t, first):
+            for v in range(RUNS):
+                edge = v % 2 == t % 2
+                nc.tensor.matmul(turned[t // 2][v // 2][:, v % 2, t % 2, :], lhsT=src[:, v * SUB : (v + 1) * SUB], rhs=ident[:], is_transpose=True,
+                                 start=first and edge and t % 2 == 0, stop=not first and edge and t % 2 == 1)
+
+        for t in range(PACK):
+            turn(y_win[t], t, True)
+
+        h1 = [keep.tile([P, S], F32, name=f"h1_{t}") for t in range(PACK)]
+        for t in range(PACK):
+            nc.vector.tensor_copy(h1[t][:], y_win[t][:].indirect(p1_sb[:]))
+        quantize_w("w2")
+        hs = keep.tile([P, PACK, S], F32, name="w2_raw", align_bytes=64)
+        for t in range(PACK):
+            nc.vector.tensor_tensor(hs[:, t, :], y_win[t][:].indirect(p2_sb[:]), h1[t][:], ADD)
+            turn(hs[:, t, :], t, False)
+        for n in ("w3", "w4"):
+            quantize_w(n)
+
+        late = keep.tile([P, 2 * PACK * S], BF16, name="w4_raw", align_bytes=64)
+        zt_all = late[:, 0 : PACK * S]
+        wide = HALF * PACK
+        z_in = [late[:, 2 * wide : 3 * wide], keep.tile([P, wide], BF16, name="z_in1", align_bytes=64)[:]]
         out_rows = out.rearrange("(a p) j -> p a j", p=P)
-        first_tags = ("h1_0", "h1_1", "w2_raw")
-        sum_tags = ("hs_0", "hs_1", "z_bf0")
-        h1, hs, z_bf = {}, {}, {}
 
-        def fetch_first(b):
-            j0, width = BLOCKS[b]
-            h1[b] = keep.tile([P, PACK, width], F32, name=first_tags[b])
+        def product(v, dst):
+            cols = slice(v * SUB, (v + 1) * SUB)
+            own = bank(C_BANKS[v], [P, PACK, SUB])
             for t in range(PACK):
-                nc.vector.tensor_copy(h1[b][:, t, :], y_win[t][:].indirect(p1_sb[:, list_columns(j0, width)]))
-
-        def fetch_second(b):
-            j0, width = BLOCKS[b]
-            hs[b] = keep.tile([P, PACK, width], F32, name=sum_tags[b], align_bytes=64)
-            for t in range(PACK):
-                nc.vector.tensor_tensor(hs[b][:, t, :], y_win[t][:].indirect(p2_sb[:, list_columns(j0, width)]), h1[b][:, t, :], ADD)
-
-        def with_own(b, n, which, op, u, own):
-            j0, width = BLOCKS[b]
-            cols = slice(j0 + u * SUB, j0 + (u + 1) * SUB)
-            for t in range(PACK):
-                mm(own[:, t, :], n, t, xw[:, cols], xs[:, cols], True, True)
-            first = (which * width + u * SUB) * PACK
+                mm(own[:, t, :], "w2", t, xw[:, cols], xs[:, cols], True, True)
             nc.vector.tensor_tensor(
-                z_bf[b][:, first : first + SUB * PACK].rearrange("p (c i t) -> p c t i", i=2, t=PACK),
+                dst.rearrange("p (c i t) -> p c t i", i=2, t=PACK),
                 own[:].rearrange("p t (c i) -> p c t i", i=2),
-                hs[b][:, :, u * SUB : (u + 1) * SUB].rearrange("p t (c i) -> p c t i", i=2),
-                op,
+                hs[:, :, cols].rearrange("p t (c i) -> p c t i", i=2),
+                MULT,
             )
 
-        def sum_turned(b):
-            j0, width = BLOCKS[b]
-            subs = width // SUB
-            back = bank(BACK_BANKS[b], [P, subs, 2, SUB])
-            for u in range(subs):
-                v = j0 // SUB + u
-                for t in range(PACK):
-                    nc.tensor.matmul(turned[v][:, t, :], lhsT=hs[b][:, t, u * SUB : (u + 1) * SUB], rhs=ident[:], is_transpose=True, start=False, stop=t == PACK - 1)
-                zt_bf = zt_all[:, v * SUB * PACK : (v + 1) * SUB * PACK]
-                nc.scalar.copy(out=zt_bf.rearrange("k (h p e) -> k h p e", h=2, e=2), in_=turned[v][:].rearrange("k (h e) p -> k h p e", e=2))
-                for h in range(2):
-                    nc.tensor.transpose(back[:, u, h, :], zt_bf.bitcast(F32)[:, h * P : (h + 1) * P], ident[:])
-            nc.scalar.copy(out=z_bf[b][:, 0 : width * PACK].bitcast(F32).rearrange("p (u k h) -> p u k h", u=subs, h=2),
-                           in_=back[:].rearrange("p u h k -> p u k h"))
+        back = {}
 
-        def finish(b):
-            j0, width = BLOCKS[b]
-            z_codes = keep.tile([P, 2, width], U32, name=f"z_codes{b}", align_bytes=64)
-            z_scale = keep.tile([P, 2, width], U8, name=f"z_scale{b}", align_bytes=64)
-            res = keep.tile([P, PACK, width], F32, name=f"res{b}")
-            if b == LAST:
-                for which in range(2):
-                    nc.vector.quantize_mx(out=z_codes[:, which, :].bitcast(FP8X4), scales=z_scale[:, which, :],
-                                          in_=z_bf[b][:, which * width * PACK : (which + 1) * width * PACK])
-                accs = [bank(index, [P, width]) for index in LAST_OUT_BANKS]
+        def turn_back(h, b):
+            if h == 0:
+                back[b] = bank(BACK_BANKS[b], [P, 2, 2, SUB])
+            first = (2 * h + b) * 4 * SUB
+            zt_bf = zt_all[:, first : first + 4 * SUB]
+            nc.scalar.copy(out=zt_bf.rearrange("k (u p e) -> k u p e", u=2, e=2), in_=turned[h][b][:].rearrange("k u e p -> k u p e"))
+            for u in range(2):
+                nc.tensor.transpose(back[b][:, u, h, :], zt_bf.bitcast(F32)[:, u * P : (u + 1) * P], ident[:])
+            if h == 1:
+                nc.scalar.copy(out=z_in[b].bitcast(F32).rearrange("p (u k h) -> p u k h", u=2, h=2), in_=back[b][:].rearrange("p u h k -> p u k h"))
+
+        def quantize_z(name, src):
+            width = src.shape[1] // PACK
+            codes = keep.tile([P, width], U32, name=f"{name}_codes", align_bytes=64)
+            scale = keep.tile([P, width], U8, name=f"{name}_scale", align_bytes=64)
+            nc.vector.quantize_mx(out=codes[:].bitcast(FP8X4), scales=scale[:], in_=src)
+            return codes, scale
+
+        res = keep.tile([P, PACK, S], F32, name="res")
+        both = late[:, 2 * wide : 4 * wide]
+        product(0, both[:, wide : wide + SUB * PACK])
+        product(1, both[:, wide + SUB * PACK : 2 * wide])
+        turn_back(0, 0)
+        turn_back(0, 1)
+        turn_back(1, 0)
+        codes, scale = quantize_z("first", both)
+        turn_back(1, 1)
+        z2_third = keep.tile([P, SUB * PACK], BF16, name="z2_third", align_bytes=64)
+        product(2, z2_third[:])
+        for g in range(2):
+            acc = bank(OUT_BANKS[0][g], [P, 2, HALF])
+            for a in range(2):
                 for which, n in enumerate(("w3", "w4")):
-                    for a in range(PACK):
-                        mm(accs[a][:], n, a, z_codes[:, which, :], z_scale[:, which, :], which == 0, which == 1)
-                for a in range(PACK):
-                    copy = nc.vector.tensor_copy if a % 2 == 1 else nc.scalar.copy
-                    copy(out=res[:, a, :], in_=accs[a][:])
-                nc.sync.dma_start(out=out_rows[:, 0:2, j0 : j0 + width], in_=res[:, 0:2, :])
-                nc.scalar.dma_start(out=out_rows[:, 2:4, j0 : j0 + width], in_=res[:, 2:4, :])
-            else:
-                nc.vector.quantize_mx(out=z_codes[:].rearrange("p a n -> p (a n)").bitcast(FP8X4),
-                                      scales=z_scale[:].rearrange("p a n -> p (a n)"), in_=z_bf[b][:])
-                per_bank = S // width
-                for g in range(PACK // per_bank):
-                    acc = bank(j0 // SUB + g, [P, per_bank, width])
-                    for a in range(per_bank):
-                        for which, n in enumerate(("w3", "w4")):
-                            mm(acc[:, a, :], n, g * per_bank + a, z_codes[:, which, :], z_scale[:, which, :], which == 0, which == 1)
-                    rows_g = slice(g * per_bank, (g + 1) * per_bank)
-                    nc.scalar.copy(out=res[:, rows_g, :], in_=acc[:])
-                    nc.sync.dma_start(out=out_rows[:, rows_g, j0 : j0 + width], in_=res[:, rows_g, :])
-
-        for b, (j0, width) in enumerate(BLOCKS):
-            z_bf[b] = keep.tile([P, 2 * width * PACK], BF16, name=f"z_bf{b}", align_bytes=64)
-        for b in range(LAST):
-            fetch_first(b)
-        for b in range(LAST):
-            fetch_second(b)
-        quantize_w("w2")
-        fetch_first(LAST)
-        for b in range(LAST):
-            sum_turned(b)
-        for b in range(LAST):
-            j0, width = BLOCKS[b]
-            for u in range(width // SUB):
-                with_own(b, "w2", 1, MULT, u, bank(j0 // SUB + u, [P, PACK, SUB]))
-        quantize_w("w3")
-        quantize_w("w4")
-        for b in range(LAST):
-            finish(b)
-        fetch_second(LAST)
-        with_own(LAST, "w1", 0, ADD, 0, bank(LAST_Y_BANK, [P, PACK, SUB]))
-        with_own(LAST, "w2", 1, MULT, 0, bank(LAST_C_BANK, [P, PACK, SUB]))
-        finish(LAST)
+                    cols = slice(which * HALF, (which + 1) * HALF)
+                    mm(acc[:, a, :], n, 2 * g + a, codes[:, cols], scale[:, cols], which == 0, which == 1)
+            nc.scalar.copy(out=res[:, 2 * g : 2 * g + 2, 0:HALF], in_=acc[:])
+            nc.sync.dma_start(out=out_rows[:, 2 * g : 2 * g + 2, 0:HALF], in_=res[:, 2 * g : 2 * g + 2, 0:HALF])
+        zc, zs = quantize_z("second", z_in[1])
+        z2c, z2s = quantize_z("third", z2_third[:])
+        acc = bank(OUT_BANKS[1][0], [P, PACK, SUB])
+        for a in range(PACK):
+            mm(acc[:, a, :], "w3", a, zc[:, 0:SUB], zs[:, 0:SUB], True, False)
+            mm(acc[:, a, :], "w4", a, z2c[:], z2s[:], False, True)
+        third = slice(HALF, HALF + SUB)
+        nc.scalar.copy(out=res[:, :, third], in_=acc[:])
+        nc.sync.dma_start(out=out_rows[:, :, third], in_=res[:, :, third])
+        z2_last = keep.tile([P, SUB * PACK], BF16, name="w4_raw", align_bytes=64)
+        product(3, z2_last[:])
+        accs = [bank(index, [P, SUB]) for index in OUT_BANKS[2]]
+        for a in range(PACK):
+            mm(accs[a][:], "w3", a, zc[:, SUB:HALF], zs[:, SUB:HALF], True, False)
+        z2c, z2s = quantize_z("last", z2_last[:])
+        last = slice(HALF + SUB, S)
+        for a in range(PACK):
+            mm(accs[a][:], "w4", a, z2c[:], z2s[:], False, True)
+        for a in range(PACK):
+            copy = nc.scalar.copy if a % 2 == 1 else nc.vector.tensor_copy
+            copy(out=res[:, a, last], in_=accs[a][:])
+        nc.sync.dma_start(out=out_rows[:, 0:2, last], in_=res[:, 0:2, last])
+        nc.scalar.dma_start(out=out_rows[:, 2:4, last], in_=res[:, 2:4, last])

@@ -62,9 +62,13 @@ def tile_picked_ngcf8_none_p_kernel(tc, x_words, x_scales, w1, w2, w3, w4, offs,
         w1_raw = keep.tile([P, PACK, H], F32, name="w1_raw")
         nc.sync.dma_start(out=w1_raw[:], in_=rows(w1))
         nc.sync.dma_start(p1_sb[:], p1)
+        hs_row = keep.tile([P, 6 * S], F32, name="hs_row", align_bytes=64)
         w_raw = {}
         for name, w in (("w2", w2), ("w3", w3), ("w4", w4)):
-            w_raw[name] = keep.tile([P, PACK, H], F32, name=f"{name}_raw", align_bytes=64)
+            if name == "w2":
+                w_raw[name] = hs_row[:, 2 * S : 6 * S].rearrange("p (j c) -> p j c", j=PACK)
+            else:
+                w_raw[name] = keep.tile([P, PACK, H], F32, name=f"{name}_raw", align_bytes=64)
             if name == "w4":
                 nc.sync.dma_start(p2_sb[:], p2)
             nc.sync.dma_start(out=w_raw[name][:], in_=rows(w))
@@ -72,7 +76,7 @@ def tile_picked_ngcf8_none_p_kernel(tc, x_words, x_scales, w1, w2, w3, w4, offs,
         ident = keep.tile([P, P], F32, name="ident")
         make_identity(nc, ident[:])
         names = ("w1", "w2", "w3", "w4")
-        w_bf = {n: keep.tile([P, PACK * H], BF16, name=f"{n}_bf", align_bytes=64) for n in names}
+        w_bf = {n: keep.tile([P, PACK * H], BF16, name=f"{n}_bf", align_bytes=64) for n in names if n != "w2"}
         w_codes = {n: keep.tile([P, H], U32, name=f"{n}_codes", align_bytes=64) for n in names}
         w_scale = {n: keep.tile([P, H], U8, name=f"{n}_scale", align_bytes=64) for n in names}
 
@@ -109,13 +113,14 @@ def tile_picked_ngcf8_none_p_kernel(tc, x_words, x_scales, w1, w2, w3, w4, offs,
             cols = slice(j0, j0 + width)
             acc = bank(index % Y_BANKS, [P, width])
             mm(acc[:], "w1", t, xw[:, cols], xs[:, cols], True, True)
-            nc.scalar.copy(out=y_win[t][:, cols], in_=acc[:])
+            copy = nc.vector.tensor_copy if index == 0 else nc.scalar.copy
+            copy(out=y_win[t][:, cols], in_=acc[:])
 
-        for h in range(2):
-            cast_dealt(nc.scalar.copy, "w2", w_raw["w2"], h)
+        w_bf["w2"] = keep.tile([P, PACK * H], BF16, name="w1_codes", align_bytes=64)
+        nc.scalar.copy(out=w_bf["w2"][:].rearrange("p (t m j) -> p m j t", t=PACK, j=PACK), in_=w_raw["w2"].rearrange("p j (m t) -> p m j t", t=PACK))
         for n in ("w3", "w4"):
-            nc.scalar.copy(out=w_bf[n][:].rearrange("p (c i j) -> p c j i", i=2, j=PACK),
-                           in_=w_raw[n][:].rearrange("p j (c i) -> p c j i", i=2))
+            nc.scalar.copy(out=w_bf[n][:].rearrange("p (c i j) -> p c j i", i=4, j=PACK),
+                           in_=w_raw[n][:].rearrange("p j (c i) -> p c j i", i=4))
 
         turned = [[bank(TURN_BANKS[h][b], [P, 2, 2, SUB]) for b in range(2)] for h in range(2)]
 
@@ -131,9 +136,10 @@ def tile_picked_ngcf8_none_p_kernel(tc, x_words, x_scales, w1, w2, w3, w4, offs,
         h1 = [keep.tile([P, S], F32, name=f"h1_{t}") for t in range(PACK)]
         for t in range(PACK):
             nc.vector.tensor_copy(h1[t][:], y_win[t][:].indirect(p1_sb[:]))
-        quantize_w("w2")
-        hs = keep.tile([P, PACK, S], F32, name="w2_raw", align_bytes=64)
+        hs = hs_row[:, 0 : PACK * S].rearrange("p (t s) -> p t s", t=PACK)
         for t in range(PACK):
+            if t == 2:
+                quantize_w("w2")
             nc.vector.tensor_tensor(hs[:, t, :], y_win[t][:].indirect(p2_sb[:]), h1[t][:], ADD)
             turn(hs[:, t, :], t, False)
         for n in ("w3", "w4"):
@@ -168,6 +174,7 @@ def tile_picked_ngcf8_none_p_kernel(tc, x_words, x_scales, w1, w2, w3, w4, offs,
             for u in range(2):
                 nc.tensor.transpose(back[b][:, u, h, :], zt_bf.bitcast(F32)[:, u * P : (u + 1) * P], ident[:])
             if h == 1:
+                mm(bank(TURN_BANKS[h][b], [P, S])[:], "w2", 0, xw[:], xs[:], True, True)
                 nc.scalar.copy(out=z_in[b].bitcast(F32).rearrange("p (u k h) -> p u k h", u=2, h=2), in_=back[b][:].rearrange("p u h k -> p u k h"))
 
         def quantize_z(name, src):

@@ -55,8 +55,8 @@ def tile_picked_ngcf8_none_p_kernel(tc, x_words, x_scales, w1, w2, w3, w4, offs,
         xs = keep.tile([P, S], U8, name="xs", align_bytes=64)
 
         nc.gpsimd.memset(xs_all[:].bitcast(I32), 0)
-        nc.sync.dma_start(offs_sb[:], offs)
         nc.sync.dma_start(out=xw_all[:], in_=x_words[0].rearrange("p n t -> p (n t)").bitcast(I32))
+        nc.sync.dma_start(offs_sb[:], offs)
         for r in range(4):
             nc.sync.dma_start(out=xs_all[r:P:32, :].bitcast(I32), in_=x_scales[0][r:16:4, :].bitcast(I32))
         w1_raw = keep.tile([P, PACK, H], F32, name="w1_raw")
@@ -142,8 +142,9 @@ def tile_picked_ngcf8_none_p_kernel(tc, x_words, x_scales, w1, w2, w3, w4, offs,
                 quantize_w("w2")
             nc.vector.tensor_tensor(hs[:, t, :], y_win[t][:].indirect(p2_sb[:]), h1[t][:], ADD)
             turn(hs[:, t, :], t, False)
-        for n in ("w3", "w4"):
-            quantize_w(n)
+        quantize_w("w3")
+        mm(bank(OUT_BANKS[2][1], [P, S])[:], "w3", 0, xw[:], xs[:], True, True)
+        quantize_w("w4")
 
         late = keep.tile([P, 2 * PACK * S], BF16, name="w4_raw", align_bytes=64)
         zt_all = late[:, 0 : PACK * S]

@@ -22,13 +22,15 @@ SUB = 128
 HALF = S // 2
 RUNS = S // SUB
 SHARE = 84
+LATER_SHARE = 40
 WINDOW = 2 * S
 
 Y_BANKS = 4
 TURN_BANKS = ((4, 5), (6, 7))
-C_BANKS = (0, 1, 4, 3)
+C_BANKS = (0, 1, 4, 7)
 BACK_BANKS = (4, 5)
-OUT_BANKS = ((0, 1), (6,), (7, 2, 5, 4))
+OUT_BANKS = ((0, 1), (6,), (3, 2, 5, 4))
+IDLE_BANK = 2
 
 
 def tile_picked_ngcf8_none_p_kernel(tc, x_words, x_scales, w1, w2, w3, w4, offs, p1, p2, out):
@@ -62,11 +64,11 @@ def tile_picked_ngcf8_none_p_kernel(tc, x_words, x_scales, w1, w2, w3, w4, offs,
         w1_raw = keep.tile([P, PACK, H], F32, name="w1_raw")
         nc.sync.dma_start(out=w1_raw[:], in_=rows(w1))
         nc.sync.dma_start(p1_sb[:], p1)
-        hs_row = keep.tile([P, 6 * S], F32, name="hs_row", align_bytes=64)
+        hs_row = keep.tile([P, 5 * S], F32, name="hs_row", align_bytes=64)
         w_raw = {}
         for name, w in (("w2", w2), ("w3", w3), ("w4", w4)):
             if name == "w2":
-                w_raw[name] = hs_row[:, 2 * S : 6 * S].rearrange("p (j c) -> p j c", j=PACK)
+                w_raw[name] = hs_row[:, S : 5 * S].rearrange("p (j c) -> p j c", j=PACK)
             else:
                 w_raw[name] = keep.tile([P, PACK, H], F32, name=f"{name}_raw", align_bytes=64)
             if name == "w4":
@@ -103,8 +105,8 @@ def tile_picked_ngcf8_none_p_kernel(tc, x_words, x_scales, w1, w2, w3, w4, offs,
         cast_dealt(nc.scalar.copy, "w1", w1_raw, 0, SHARE, P)
         quantize_w1(0, P)
         quantize_w1(P, 2 * P)
-        cast_dealt(nc.vector.tensor_copy, "w1", w1_raw, 1, 0, SHARE)
-        cast_dealt(nc.scalar.copy, "w1", w1_raw, 1, SHARE, P)
+        cast_dealt(nc.vector.tensor_copy, "w1", w1_raw, 1, 0, LATER_SHARE)
+        cast_dealt(nc.scalar.copy, "w1", w1_raw, 1, LATER_SHARE, P)
         quantize_w1(2 * P, 4 * P)
 
         y_win = [keep.tile([P, WINDOW], F32, name=f"y_win{t}") for t in range(PACK)]
@@ -133,30 +135,39 @@ def tile_picked_ngcf8_none_p_kernel(tc, x_words, x_scales, w1, w2, w3, w4, offs,
         for t in range(PACK):
             turn(y_win[t], t, True)
 
+        def warm_up(index):
+            mm(bank(index, [P, S])[:], "w2", 0, xw[:], xs[:], True, True)
+
+        def make_c(v):
+            cols = slice(v * SUB, (v + 1) * SUB)
+            own = bank(C_BANKS[v], [P, PACK, SUB])
+            for t in range(PACK):
+                mm(own[:, t, :], "w2", t, xw[:, cols], xs[:, cols], True, True)
+            return own
+
         h1 = [keep.tile([P, S], F32, name=f"h1_{t}") for t in range(PACK)]
         for t in range(PACK):
             nc.vector.tensor_copy(h1[t][:], y_win[t][:].indirect(p1_sb[:]))
         hs = hs_row[:, 0 : PACK * S].rearrange("p (t s) -> p t s", t=PACK)
         for t in range(PACK):
-            if t == 2:
+            if t == 1:
                 quantize_w("w2")
+                c = {v: make_c(v) for v in range(2)}
             nc.vector.tensor_tensor(hs[:, t, :], y_win[t][:].indirect(p2_sb[:]), h1[t][:], ADD)
             turn(hs[:, t, :], t, False)
+            if t > 0:
+                warm_up(IDLE_BANK)
         quantize_w("w3")
-        mm(bank(OUT_BANKS[2][1], [P, S])[:], "w3", 0, xw[:], xs[:], True, True)
-        quantize_w("w4")
 
-        late = keep.tile([P, 2 * PACK * S], BF16, name="w4_raw", align_bytes=64)
-        zt_all = late[:, 0 : PACK * S]
+        zt_all = keep.tile([P, PACK * S], BF16, name="w4_raw", align_bytes=64)
         wide = HALF * PACK
-        z_in = [late[:, 2 * wide : 3 * wide], keep.tile([P, wide], BF16, name="z_in1", align_bytes=64)[:]]
+        both = keep.tile([P, 2 * wide], BF16, name="w3_raw", align_bytes=64)
+        z_in = [both[:, 0:wide], keep.tile([P, wide], BF16, name="z_in1", align_bytes=64)[:]]
         out_rows = out.rearrange("(a p) j -> p a j", p=P)
 
         def product(v, dst):
             cols = slice(v * SUB, (v + 1) * SUB)
-            own = bank(C_BANKS[v], [P, PACK, SUB])
-            for t in range(PACK):
-                mm(own[:, t, :], "w2", t, xw[:, cols], xs[:, cols], True, True)
+            own = c[v] if v in c else make_c(v)
             nc.vector.tensor_tensor(
                 dst.rearrange("p (c i t) -> p c t i", i=2, t=PACK),
                 own[:].rearrange("p t (c i) -> p c t i", i=2),
@@ -175,7 +186,10 @@ def tile_picked_ngcf8_none_p_kernel(tc, x_words, x_scales, w1, w2, w3, w4, offs,
             for u in range(2):
                 nc.tensor.transpose(back[b][:, u, h, :], zt_bf.bitcast(F32)[:, u * P : (u + 1) * P], ident[:])
             if h == 1:
-                mm(bank(TURN_BANKS[h][b], [P, S])[:], "w2", 0, xw[:], xs[:], True, True)
+                if b == 0:
+                    warm_up(TURN_BANKS[h][b])
+                else:
+                    c[3] = make_c(3)
                 nc.scalar.copy(out=z_in[b].bitcast(F32).rearrange("p (u k h) -> p u k h", u=2, h=2), in_=back[b][:].rearrange("p u h k -> p u k h"))
 
         def quantize_z(name, src):
@@ -186,13 +200,13 @@ def tile_picked_ngcf8_none_p_kernel(tc, x_words, x_scales, w1, w2, w3, w4, offs,
             return codes, scale
 
         res = keep.tile([P, PACK, S], F32, name="res")
-        both = late[:, 2 * wide : 4 * wide]
         product(0, both[:, wide : wide + SUB * PACK])
         product(1, both[:, wide + SUB * PACK : 2 * wide])
+        quantize_w("w4")
         turn_back(0, 0)
         turn_back(0, 1)
         turn_back(1, 0)
-        codes, scale = quantize_z("first", both)
+        codes, scale = quantize_z("first", both[:])
         turn_back(1, 1)
         z2_third = keep.tile([P, SUB * PACK], BF16, name="z2_third", align_bytes=64)
         product(2, z2_third[:])

@@ -31,12 +31,14 @@ C_BANKS = (0, 1, 4, 7)
 BACK_BANKS = (4, 5)
 OUT_BANKS = ((0, 1), (6,), (3, 2, 5, 4))
 IDLE_BANK = 2
+KIB = 1024
 
 
 def tile_picked_ngcf8_none_p_kernel(tc, x_words, x_scales, w1, w2, w3, w4, offs, p1, p2, out):
     nc = tc.nc
     with ExitStack() as ctx:
         keep = ctx.enter_context(tc.tile_pool(name="keep", bufs=1))
+        shared = ctx.enter_context(tc.tile_pool(name="shared", bufs=1))
         psum = ctx.enter_context(tc.psum_pool(name="psum", bufs=1))
 
         def bank(index, shape):
@@ -45,6 +47,9 @@ def tile_picked_ngcf8_none_p_kernel(tc, x_words, x_scales, w1, w2, w3, w4, offs,
         def list_columns(j0, width):
             return slice(j0 // 16, (j0 + width) // 16)
 
+        def placed(name, shape, dtype, kib):
+            return shared.tile(shape, dtype, name=name, offset=kib * KIB, align_bytes=64)
+
         def rows(w):
             return w.rearrange("(p j) c -> p j c", j=PACK)
 
@@ -52,27 +57,30 @@ def tile_picked_ngcf8_none_p_kernel(tc, x_words, x_scales, w1, w2, w3, w4, offs,
         p1_sb = keep.tile([P, S // 16], U16, name="p1_sb")
         p2_sb = keep.tile([P, S // 16], U16, name="p2_sb")
         xw_all = keep.tile([P, T], I32, name="xw_all", align_bytes=64)
-        xs_all = keep.tile([P, T], U8, name="xs_all", align_bytes=64)
+        xs_all = placed("xs_all", [P, T], U8, 9)
         xw = keep.tile([P, S], U32, name="xw", align_bytes=64)
+        xs_apart = keep.tile([P, S], U8, name="w4_raw", align_bytes=64)
         xs = keep.tile([P, S], U8, name="xs", align_bytes=64)
 
-        nc.gpsimd.memset(xs_all[:].bitcast(I32), 0)
-        nc.sync.dma_start(out=xw_all[:], in_=x_words[0].rearrange("p n t -> p (n t)").bitcast(I32))
+        nc.gpsimd.memset(xs_all[96:112, :].bitcast(I32), 0)
+        nc.vector.memset(xs_all[0:96, :].bitcast(I32), 0)
+        nc.gpsimd.memset(xs[:].bitcast(I32), 0)
+        nc.sync.dma_start(out=xs_all[112:P, :].bitcast(I32), in_=x_scales[0].bitcast(I32))
         nc.sync.dma_start(offs_sb[:], offs)
-        for r in range(4):
-            nc.sync.dma_start(out=xs_all[r:P:32, :].bitcast(I32), in_=x_scales[0][r:16:4, :].bitcast(I32))
+        nc.sync.dma_start(p1_sb[:], p1)
+        nc.sync.dma_start(out=xw_all[:], in_=x_words[0].rearrange("p n t -> p (n t)").bitcast(I32))
         w1_raw = keep.tile([P, PACK, H], F32, name="w1_raw")
         nc.sync.dma_start(out=w1_raw[:], in_=rows(w1))
-        nc.sync.dma_start(p1_sb[:], p1)
-        hs_row = keep.tile([P, 5 * S], F32, name="hs_row", align_bytes=64)
-        w_raw = {}
-        for name, w in (("w2", w2), ("w3", w3), ("w4", w4)):
-            if name == "w2":
-                w_raw[name] = hs_row[:, S : 5 * S].rearrange("p (j c) -> p j c", j=PACK)
-            else:
-                w_raw[name] = keep.tile([P, PACK, H], F32, name=f"{name}_raw", align_bytes=64)
-            if name == "w4":
-                nc.sync.dma_start(p2_sb[:], p2)
+        nc.sync.dma_start(p2_sb[:], p2)
+        nc.vector.tensor_copy(xs_apart[:], xs_all[:].indirect(offs_sb[:]))
+        for r in range(4):
+            nc.sync.dma_start(out=xs[r:P:32, :].bitcast(I32), in_=xs_apart[112 + r : P : 4, :].bitcast(I32))
+        hs_row = placed("hs_row", [P, 5 * S], F32, 0)
+        w2_raw = [hs_row[:, first : first + 2 * S].rearrange("p (j c) -> p j c", j=PACK) for first in (0, 2 * S + HALF)]
+        for g in range(2):
+            nc.sync.dma_start(out=w2_raw[g], in_=rows(w2)[:, :, g * HALF : (g + 1) * HALF])
+        w_raw = {"w3": placed("w3_raw", [P, PACK, H], F32, 10), "w4": keep.tile([P, PACK, H], F32, name="w4_raw", align_bytes=64)}
+        for name, w in (("w3", w3), ("w4", w4)):
             nc.sync.dma_start(out=w_raw[name][:], in_=rows(w))
 
         ident = keep.tile([P, P], F32, name="ident")
@@ -96,7 +104,6 @@ def tile_picked_ngcf8_none_p_kernel(tc, x_words, x_scales, w1, w2, w3, w4, offs,
                                 rhs=codes.bitcast(FP8X4), rhs_scale=scales, start=start, stop=stop)
 
         nc.vector.tensor_copy(xw[:], xw_all[:].bitcast(U32).indirect(offs_sb[:]))
-        nc.vector.tensor_copy(xs[:], xs_all[:].indirect(offs_sb[:]))
 
         def quantize_w1(c0, c1):
             nc.vector.quantize_mx(out=w_codes["w1"][:, c0:c1].bitcast(FP8X4), scales=w_scale["w1"][:, c0:c1], in_=w_bf["w1"][:, PACK * c0 : PACK * c1])
@@ -119,7 +126,9 @@ def tile_picked_ngcf8_none_p_kernel(tc, x_words, x_scales, w1, w2, w3, w4, offs,
             copy(out=y_win[t][:, cols], in_=acc[:])
 
         w_bf["w2"] = keep.tile([P, PACK * H], BF16, name="w1_codes", align_bytes=64)
-        nc.scalar.copy(out=w_bf["w2"][:].rearrange("p (t m j) -> p m j t", t=PACK, j=PACK), in_=w_raw["w2"].rearrange("p j (m t) -> p m j t", t=PACK))
+        for g in range(2):
+            nc.scalar.copy(out=w_bf["w2"][:].rearrange("p (t m j) -> p m j t", t=PACK, j=PACK)[:, g * P // 2 : (g + 1) * P // 2],
+                           in_=w2_raw[g].rearrange("p j (m t) -> p m j t", t=PACK))
         for n in ("w3", "w4"):
             nc.scalar.copy(out=w_bf[n][:].rearrange("p (c i j) -> p c j i", i=4, j=PACK),
                            in_=w_raw[n][:].rearrange("p j (c i) -> p c j i", i=4))
@@ -148,7 +157,7 @@ def tile_picked_ngcf8_none_p_kernel(tc, x_words, x_scales, w1, w2, w3, w4, offs,
         h1 = [keep.tile([P, S], F32, name=f"h1_{t}") for t in range(PACK)]
         for t in range(PACK):
             nc.vector.tensor_copy(h1[t][:], y_win[t][:].indirect(p1_sb[:]))
-        hs = hs_row[:, 0 : PACK * S].rearrange("p (t s) -> p t s", t=PACK)
+        hs = hs_row[:, S : 5 * S].rearrange("p (t s) -> p t s", t=PACK)
         for t in range(PACK):
             if t == 1:
                 quantize_w("w2")
@@ -161,7 +170,7 @@ def tile_picked_ngcf8_none_p_kernel(tc, x_words, x_scales, w1, w2, w3, w4, offs,
 
         zt_all = keep.tile([P, PACK * S], BF16, name="w4_raw", align_bytes=64)
         wide = HALF * PACK
-        both = keep.tile([P, 2 * wide], BF16, name="w3_raw", align_bytes=64)
+        both = placed("both", [P, 2 * wide], BF16, 12)
         z_in = [both[:, 0:wide], keep.tile([P, wide], BF16, name="z_in1", align_bytes=64)[:]]
         out_rows = out.rearrange("(a p) j -> p a j", p=P)
 

@@ -48,7 +48,7 @@ def tile_picked_ngcf8_none_p_kernel(tc, x_words, x_scales, w1, w2, w3, w4, offs,
             return slice(j0 // 16, (j0 + width) // 16)
 
         def placed(name, shape, dtype, kib):
-            return shared.tile(shape, dtype, name=name, offset=kib * KIB, align_bytes=64)
+            return shared.tile(shape, dtype, name=name, offset=int(kib * KIB), align_bytes=64)
 
         def rows(w):
             return w.rearrange("(p j) c -> p j c", j=PACK)
@@ -57,9 +57,9 @@ def tile_picked_ngcf8_none_p_kernel(tc, x_words, x_scales, w1, w2, w3, w4, offs,
         p1_sb = keep.tile([P, S // 16], U16, name="p1_sb")
         p2_sb = keep.tile([P, S // 16], U16, name="p2_sb")
         xw_all = keep.tile([P, T], I32, name="xw_all", align_bytes=64)
-        xs_all = placed("xs_all", [P, T], U8, 9)
+        xs_all = keep.tile([P, T], U8, name="xs_all", align_bytes=64)
         xw = keep.tile([P, S], U32, name="xw", align_bytes=64)
-        xs_apart = keep.tile([P, S], U8, name="w4_raw", align_bytes=64)
+        xs_apart = placed("xs_apart", [P, S], U8, 9.75)
         xs = keep.tile([P, S], U8, name="xs", align_bytes=64)
 
         nc.gpsimd.memset(xs_all[96:112, :].bitcast(I32), 0)
@@ -74,14 +74,13 @@ def tile_picked_ngcf8_none_p_kernel(tc, x_words, x_scales, w1, w2, w3, w4, offs,
         nc.sync.dma_start(p2_sb[:], p2)
         nc.vector.tensor_copy(xs_apart[:], xs_all[:].indirect(offs_sb[:]))
         for r in range(4):
-            nc.sync.dma_start(out=xs[r:P:32, :].bitcast(I32), in_=xs_apart[112 + r : P : 4, :].bitcast(I32))
+            nc.scalar.dma_start(out=xs[r:P:32, :].bitcast(I32), in_=xs_apart[112 + r : P : 4, :].bitcast(I32))
         hs_row = placed("hs_row", [P, 5 * S], F32, 0)
         w2_raw = [hs_row[:, first : first + 2 * S].rearrange("p (j c) -> p j c", j=PACK) for first in (0, 2 * S + HALF)]
         for g in range(2):
             nc.sync.dma_start(out=w2_raw[g], in_=rows(w2)[:, :, g * HALF : (g + 1) * HALF])
-        w_raw = {"w3": placed("w3_raw", [P, PACK, H], F32, 10), "w4": keep.tile([P, PACK, H], F32, name="w4_raw", align_bytes=64)}
-        for name, w in (("w3", w3), ("w4", w4)):
-            nc.sync.dma_start(out=w_raw[name][:], in_=rows(w))
+        w_raw = {"w3": placed("w3_raw", [P, PACK, H], F32, 10)}
+        nc.sync.dma_start(out=w_raw["w3"][:], in_=rows(w3))
 
         ident = keep.tile([P, P], F32, name="ident")
         make_identity(nc, ident[:])
@@ -115,6 +114,9 @@ def tile_picked_ngcf8_none_p_kernel(tc, x_words, x_scales, w1, w2, w3, w4, offs,
         cast_dealt(nc.vector.tensor_copy, "w1", w1_raw, 1, 0, LATER_SHARE)
         cast_dealt(nc.scalar.copy, "w1", w1_raw, 1, LATER_SHARE, P)
         quantize_w1(2 * P, 4 * P)
+
+        w_raw["w4"] = keep.tile([P, PACK, H], F32, name="w1_bf", align_bytes=64)
+        nc.sync.dma_start(out=w_raw["w4"][:], in_=rows(w4))
 
         y_win = [keep.tile([P, WINDOW], F32, name=f"y_win{t}") for t in range(PACK)]
         pieces = [(0, 0, HALF), (0, HALF, HALF)] + [(t, 0, S) for t in range(1, PACK)]
@@ -168,7 +170,7 @@ def tile_picked_ngcf8_none_p_kernel(tc, x_words, x_scales, w1, w2, w3, w4, offs,
                 warm_up(IDLE_BANK)
         quantize_w("w3")
 
-        zt_all = keep.tile([P, PACK * S], BF16, name="w4_raw", align_bytes=64)
+        zt_all = keep.tile([P, PACK * S], BF16, name="w1_bf", align_bytes=64)
         wide = HALF * PACK
         both = placed("both", [P, 2 * wide], BF16, 12)
         z_in = [both[:, 0:wide], keep.tile([P, wide], BF16, name="z_in1", align_bytes=64)[:]]
@@ -236,7 +238,7 @@ def tile_picked_ngcf8_none_p_kernel(tc, x_words, x_scales, w1, w2, w3, w4, offs,
         third = slice(HALF, HALF + SUB)
         nc.scalar.copy(out=res[:, :, third], in_=acc[:])
         nc.sync.dma_start(out=out_rows[:, :, third], in_=res[:, :, third])
-        z2_last = keep.tile([P, SUB * PACK], BF16, name="w4_raw", align_bytes=64)
+        z2_last = keep.tile([P, SUB * PACK], BF16, name="w1_bf", align_bytes=64)
         product(3, z2_last[:])
         accs = [bank(index, [P, SUB]) for index in OUT_BANKS[2]]
         for a in range(PACK):

@@ -22,14 +22,14 @@ SUB = 128
 HALF = S // 2
 RUNS = S // SUB
 SHARE = 84
-LATER_SHARE = 40
+EARLY_SHARE = 96
 WINDOW = 2 * S
 
 Y_BANKS = 4
 TURN_BANKS = ((4, 5), (6, 7))
 C_BANKS = (0, 1, 4, 7)
 BACK_BANKS = (4, 5)
-OUT_BANKS = ((0, 1), (6,), (3, 2, 5, 4))
+OUT_BANKS = ((0, 1, 3, 2), (6, 4), (0, 1, 5, 3))
 IDLE_BANK = 2
 KIB = 1024
 
@@ -67,10 +67,11 @@ def tile_picked_ngcf8_none_p_kernel(tc, x_words, x_scales, w1, w2, w3, w4, offs,
         nc.gpsimd.memset(xs[:].bitcast(I32), 0)
         nc.sync.dma_start(out=xs_all[112:P, :].bitcast(I32), in_=x_scales[0].bitcast(I32))
         nc.sync.dma_start(offs_sb[:], offs)
-        nc.sync.dma_start(p1_sb[:], p1)
         nc.sync.dma_start(out=xw_all[:], in_=x_words[0].rearrange("p n t -> p (n t)").bitcast(I32))
-        w1_raw = keep.tile([P, PACK, H], F32, name="w1_raw")
-        nc.sync.dma_start(out=w1_raw[:], in_=rows(w1))
+        w1_raw = [keep.tile([P, 2, H], F32, name=f"w1_raw{g}") for g in range(2)]
+        for g in range(2):
+            nc.sync.dma_start(out=w1_raw[g][:], in_=rows(w1)[:, 2 * g : 2 * g + 2, :])
+        nc.sync.dma_start(p1_sb[:], p1)
         nc.sync.dma_start(p2_sb[:], p2)
         nc.vector.tensor_copy(xs_apart[:], xs_all[:].indirect(offs_sb[:]))
         for r in range(4):
@@ -91,7 +92,7 @@ def tile_picked_ngcf8_none_p_kernel(tc, x_words, x_scales, w1, w2, w3, w4, offs,
 
         def cast_dealt(copy, n, raw, h, m0=0, m1=P):
             half = w_bf[n][:, h * 2 * H : (h + 1) * 2 * H]
-            copy(out=half.rearrange("p (e m j) -> p m j e", e=2, j=PACK)[:, m0:m1],
+            copy(out=half.rearrange("p (e m j) -> p m j e", e=2, j=PACK)[:, m0:m1, 2:4],
                  in_=raw[:].rearrange("p j (m h e) -> p h m j e", h=2, e=2)[:, h, m0:m1])
 
         def quantize_w(n):
@@ -107,12 +108,13 @@ def tile_picked_ngcf8_none_p_kernel(tc, x_words, x_scales, w1, w2, w3, w4, offs,
         def quantize_w1(c0, c1):
             nc.vector.quantize_mx(out=w_codes["w1"][:, c0:c1].bitcast(FP8X4), scales=w_scale["w1"][:, c0:c1], in_=w_bf["w1"][:, PACK * c0 : PACK * c1])
 
-        cast_dealt(nc.vector.tensor_copy, "w1", w1_raw, 0, 0, SHARE)
-        cast_dealt(nc.scalar.copy, "w1", w1_raw, 0, SHARE, P)
+        for copy, m0, m1 in ((nc.vector.tensor_copy, 0, EARLY_SHARE), (nc.scalar.copy, EARLY_SHARE, P)):
+            copy(out=w_bf["w1"][:].rearrange("p (t m j) -> p m j t", t=PACK, j=PACK)[:, m0:m1, 0:2], in_=w1_raw[0][:].rearrange("p j (m t) -> p m j t", t=PACK)[:, m0:m1])
+        cast_dealt(nc.vector.tensor_copy, "w1", w1_raw[1], 0, 0, SHARE)
+        cast_dealt(nc.scalar.copy, "w1", w1_raw[1], 0, SHARE, P)
         quantize_w1(0, P)
         quantize_w1(P, 2 * P)
-        cast_dealt(nc.vector.tensor_copy, "w1", w1_raw, 1, 0, LATER_SHARE)
-        cast_dealt(nc.scalar.copy, "w1", w1_raw, 1, LATER_SHARE, P)
+        cast_dealt(nc.scalar.copy, "w1", w1_raw[1], 1)
         quantize_w1(2 * P, 4 * P)
 
         w_raw["w4"] = keep.tile([P, PACK, H], F32, name="w1_bf", align_bytes=64)
@@ -221,23 +223,23 @@ def tile_picked_ngcf8_none_p_kernel(tc, x_words, x_scales, w1, w2, w3, w4, offs,
         turn_back(1, 1)
         z2_third = keep.tile([P, SUB * PACK], BF16, name="z2_third", align_bytes=64)
         product(2, z2_third[:])
-        for g in range(2):
-            acc = bank(OUT_BANKS[0][g], [P, 2, HALF])
-            for a in range(2):
-                for which, n in enumerate(("w3", "w4")):
-                    cols = slice(which * HALF, (which + 1) * HALF)
-                    mm(acc[:, a, :], n, 2 * g + a, codes[:, cols], scale[:, cols], which == 0, which == 1)
-            nc.scalar.copy(out=res[:, 2 * g : 2 * g + 2, 0:HALF], in_=acc[:])
-            nc.sync.dma_start(out=out_rows[:, 2 * g : 2 * g + 2, 0:HALF], in_=res[:, 2 * g : 2 * g + 2, 0:HALF])
+        for a in range(PACK):
+            acc = bank(OUT_BANKS[0][a], [P, HALF])
+            for which, n in enumerate(("w3", "w4")):
+                cols = slice(which * HALF, (which + 1) * HALF)
+                mm(acc[:], n, a, codes[:, cols], scale[:, cols], which == 0, which == 1)
+            nc.scalar.copy(out=res[:, a, 0:HALF], in_=acc[:])
+            nc.sync.dma_start(out=out_rows[:, a, 0:HALF], in_=res[:, a, 0:HALF])
         zc, zs = quantize_z("second", z_in[1])
         z2c, z2s = quantize_z("third", z2_third[:])
-        acc = bank(OUT_BANKS[1][0], [P, PACK, SUB])
-        for a in range(PACK):
-            mm(acc[:, a, :], "w3", a, zc[:, 0:SUB], zs[:, 0:SUB], True, False)
-            mm(acc[:, a, :], "w4", a, z2c[:], z2s[:], False, True)
         third = slice(HALF, HALF + SUB)
-        nc.scalar.copy(out=res[:, :, third], in_=acc[:])
-        nc.sync.dma_start(out=out_rows[:, :, third], in_=res[:, :, third])
+        for g in range(2):
+            acc = bank(OUT_BANKS[1][g], [P, 2, SUB])
+            for a in range(2):
+                mm(acc[:, a, :], "w3", 2 * g + a, zc[:, 0:SUB], zs[:, 0:SUB], True, False)
+                mm(acc[:, a, :], "w4", 2 * g + a, z2c[:], z2s[:], False, True)
+            nc.scalar.copy(out=res[:, 2 * g : 2 * g + 2, third], in_=acc[:])
+            nc.sync.dma_start(out=out_rows[:, 2 * g : 2 * g + 2, third], in_=res[:, 2 * g : 2 * g + 2, third])
         z2_last = keep.tile([P, SUB * PACK], BF16, name="w1_bf", align_bytes=64)
         product(3, z2_last[:])
         accs = [bank(index, [P, SUB]) for index in OUT_BANKS[2]]

@@ -65,6 +65,9 @@ def tile_picked_ngcf8_none_p_kernel(tc, x_words, x_scales, w1, w2, w3, w4, offs,
         nc.gpsimd.memset(xs_all[96:112, :].bitcast(I32), 0)
         nc.vector.memset(xs_all[0:96, :].bitcast(I32), 0)
         nc.gpsimd.memset(xs[:].bitcast(I32), 0)
+        early = keep.tile([P, 2], F32, name="early")
+        nc.gpsimd.memset(early[:, 0:1], 0.0)
+        nc.scalar.copy(out=early[:, 1:2], in_=early[:, 0:1])
         nc.sync.dma_start(out=xs_all[112:P, :].bitcast(I32), in_=x_scales[0].bitcast(I32))
         nc.sync.dma_start(offs_sb[:], offs)
         nc.sync.dma_start(out=xw_all[:], in_=x_words[0].rearrange("p n t -> p (n t)").bitcast(I32))
@@ -121,7 +124,7 @@ def tile_picked_ngcf8_none_p_kernel(tc, x_words, x_scales, w1, w2, w3, w4, offs,
         nc.sync.dma_start(out=w_raw["w4"][:], in_=rows(w4))
 
         y_win = [keep.tile([P, WINDOW], F32, name=f"y_win{t}") for t in range(PACK)]
-        pieces = [(0, 0, HALF), (0, HALF, HALF)] + [(t, 0, S) for t in range(1, PACK)]
+        pieces = [(0, 0, HALF), (0, HALF, SUB), (0, HALF + SUB, SUB)] + [(t, 0, S) for t in range(1, PACK)]
         for index, (t, j0, width) in enumerate(pieces):
             cols = slice(j0, j0 + width)
             acc = bank(index % Y_BANKS, [P, width])

@@ -56,10 +56,10 @@ def tile_picked_ngcf8_none_p_kernel(tc, x_words, x_scales, w1, w2, w3, w4, offs,
         offs_sb = keep.tile([P, S // 16], U16, name="offs_sb")
         p1_sb = keep.tile([P, S // 16], U16, name="p1_sb")
         p2_sb = keep.tile([P, S // 16], U16, name="p2_sb")
-        xw_all = keep.tile([P, T], I32, name="xw_all", align_bytes=64)
+        xw_all = placed("xw_all", [P, T], I32, 6)
         xs_all = keep.tile([P, T], U8, name="xs_all", align_bytes=64)
         xw = keep.tile([P, S], U32, name="xw", align_bytes=64)
-        xs_apart = placed("xs_apart", [P, S], U8, 9.75)
+        xs_apart = keep.tile([P, S], U8, name="xs_apart", align_bytes=64)
         xs = keep.tile([P, S], U8, name="xs", align_bytes=64)
 
         nc.gpsimd.memset(xs_all[96:112, :].bitcast(I32), 0)

@@ -22,7 +22,7 @@ SUB = 128
 HALF = S // 2
 RUNS = S // SUB
 SHARE = 84
-EARLY_SHARE = 96
+EARLY_SHARE = 64
 WINDOW = 2 * S
 
 Y_BANKS = 4
@@ -93,6 +93,10 @@ def tile_picked_ngcf8_none_p_kernel(tc, x_words, x_scales, w1, w2, w3, w4, offs,
         w_codes = {n: keep.tile([P, H], U32, name=f"{n}_codes", align_bytes=64) for n in names}
         w_scale = {n: keep.tile([P, H], U8, name=f"{n}_scale", align_bytes=64) for n in names}
 
+        def cast_tile(copy, t, m0, m1):
+            copy(out=w_bf["w1"][:, t * H : (t + 1) * H].rearrange("p (m j) -> p m j", j=PACK)[:, m0:m1, 2:4],
+                 in_=w1_raw[1][:].rearrange("p j (m t) -> p t m j", t=PACK)[:, t, m0:m1])
+
         def cast_dealt(copy, n, raw, h, m0=0, m1=P):
             half = w_bf[n][:, h * 2 * H : (h + 1) * 2 * H]
             copy(out=half.rearrange("p (e m j) -> p m j e", e=2, j=PACK)[:, m0:m1, 2:4],
@@ -113,8 +117,9 @@ def tile_picked_ngcf8_none_p_kernel(tc, x_words, x_scales, w1, w2, w3, w4, offs,
 
         for copy, m0, m1 in ((nc.vector.tensor_copy, 0, EARLY_SHARE), (nc.scalar.copy, EARLY_SHARE, P)):
             copy(out=w_bf["w1"][:].rearrange("p (t m j) -> p m j t", t=PACK, j=PACK)[:, m0:m1, 0:2], in_=w1_raw[0][:].rearrange("p j (m t) -> p m j t", t=PACK)[:, m0:m1])
-        cast_dealt(nc.vector.tensor_copy, "w1", w1_raw[1], 0, 0, SHARE)
-        cast_dealt(nc.scalar.copy, "w1", w1_raw[1], 0, SHARE, P)
+        for t in range(2):
+            cast_tile(nc.vector.tensor_copy, t, 0, SHARE)
+            cast_tile(nc.scalar.copy, t, SHARE, P)
         quantize_w1(0, P)
         quantize_w1(P, 2 * P)
         cast_dealt(nc.scalar.copy, "w1", w1_raw[1], 1)

@@ -65,10 +65,10 @@ def tile_picked_ngcf8_none_p_kernel(tc, x_words, x_scales, w1, w2, w3, w4, offs,
         nc.gpsimd.memset(xs_all[96:112, :].bitcast(I32), 0)
         nc.vector.memset(xs_all[0:96, :].bitcast(I32), 0)
         nc.gpsimd.memset(xs[:].bitcast(I32), 0)
+        nc.scalar.dma_start(out=xs_all[112:P, :].bitcast(I32), in_=x_scales[0].bitcast(I32))
         early = keep.tile([P, 2], F32, name="early")
         nc.gpsimd.memset(early[:, 0:1], 0.0)
         nc.scalar.copy(out=early[:, 1:2], in_=early[:, 0:1])
-        nc.sync.dma_start(out=xs_all[112:P, :].bitcast(I32), in_=x_scales[0].bitcast(I32))
         nc.sync.dma_start(offs_sb[:], offs)
         nc.sync.dma_start(out=xw_all[:], in_=x_words[0].rearrange("p n t -> p (n t)").bitcast(I32))
         w1_raw = [keep.tile([P, 2, H], F32, name=f"w1_raw{g}") for g in range(2)]
@@ -80,7 +80,7 @@ def tile_picked_ngcf8_none_p_kernel(tc, x_words, x_scales, w1, w2, w3, w4, offs,
         for r in range(4):
             nc.scalar.dma_start(out=xs[r:P:32, :].bitcast(I32), in_=xs_apart[112 + r : P : 4, :].bitcast(I32))
         hs_row = placed("hs_row", [P, 5 * S], F32, 0)
-        w2_raw = [hs_row[:, first : first + 2 * S].rearrange("p (j c) -> p j c", j=PACK) for first in (0, 2 * S + HALF)]
+        w2_raw = [hs_row[:, first : first + 2 * S].rearrange("p (j c) -> p j c", j=PACK) for first in (0, 3 * S - SUB)]
         for g in range(2):
             nc.sync.dma_start(out=w2_raw[g], in_=rows(w2)[:, :, g * HALF : (g + 1) * HALF])
         w_raw = {"w3": placed("w3_raw", [P, PACK, H], F32, 10)}
@@ -147,8 +147,8 @@ def tile_picked_ngcf8_none_p_kernel(tc, x_words, x_scales, w1, w2, w3, w4, offs,
 
         turned = [[bank(TURN_BANKS[h][b], [P, 2, 2, SUB]) for b in range(2)] for h in range(2)]
 
-        def turn(src, t, first):
-            for v in range(RUNS):
+        def turn(src, t, first, runs=range(RUNS)):
+            for v in runs:
                 edge = v % 2 == t % 2
                 nc.tensor.matmul(turned[t // 2][v // 2][:, v % 2, t % 2, :], lhsT=src[:, v * SUB : (v + 1) * SUB], rhs=ident[:], is_transpose=True,
                                  start=first and edge and t % 2 == 0, stop=not first and edge and t % 2 == 1)
@@ -174,9 +174,17 @@ def tile_picked_ngcf8_none_p_kernel(tc, x_words, x_scales, w1, w2, w3, w4, offs,
             if t == 1:
                 quantize_w("w2")
                 c = {v: make_c(v) for v in range(2)}
-            nc.vector.tensor_tensor(hs[:, t, :], y_win[t][:].indirect(p2_sb[:]), h1[t][:], ADD)
-            turn(hs[:, t, :], t, False)
-            if t > 0:
+            if t < PACK - 1:
+                nc.vector.tensor_tensor(hs[:, t, :], y_win[t][:].indirect(p2_sb[:]), h1[t][:], ADD)
+                turn(hs[:, t, :], t, False)
+            else:
+                for b in range(2):
+                    cols = slice(b * HALF, (b + 1) * HALF)
+                    nc.vector.tensor_tensor(hs[:, t, cols], y_win[t][:].indirect(p2_sb[:, list_columns(b * HALF, HALF)]), h1[t][:, cols], ADD)
+                    turn(hs[:, t, :], t, False, range(2 * b, 2 * b + 2))
+                    if b == 0:
+                        warm_up(IDLE_BANK)
+            if t in (1, 2):
                 warm_up(IDLE_BANK)
         quantize_w("w3")
 

@@ -174,6 +174,7 @@ def tile_picked_ngcf8_none_p_kernel(tc, x_words, x_scales, w1, w2, w3, w4, offs,
             if t == 1:
                 quantize_w("w2")
                 c = {v: make_c(v) for v in range(2)}
+                warm_up(IDLE_BANK)
             if t < PACK - 1:
                 nc.vector.tensor_tensor(hs[:, t, :], y_win[t][:].indirect(p2_sb[:]), h1[t][:], ADD)
                 turn(hs[:, t, :], t, False)
@@ -184,7 +185,7 @@ def tile_picked_ngcf8_none_p_kernel(tc, x_words, x_scales, w1, w2, w3, w4, offs,
                     turn(hs[:, t, :], t, False, range(2 * b, 2 * b + 2))
                     if b == 0:
                         warm_up(IDLE_BANK)
-            if t in (1, 2):
+            if t == 1:
                 warm_up(IDLE_BANK)
         quantize_w("w3")
 

@@ -15,6 +15,7 @@ U8 = mybir.dt.uint8
 FP8X4 = mybir.dt.float8_e4m3fn_x4
 ADD = mybir.AluOpType.add
 MULT = mybir.AluOpType.mult
+COPY = mybir.ActivationFunctionType.Copy
 
 P = 128
 PACK = 4
@@ -71,7 +72,7 @@ def tile_picked_ngcf8_none_p_kernel(tc, x_words, x_scales, w1, w2, w3, w4, offs,
         nc.scalar.copy(out=early[:, 1:2], in_=early[:, 0:1])
         nc.sync.dma_start(offs_sb[:], offs)
         nc.sync.dma_start(out=xw_all[:], in_=x_words[0].rearrange("p n t -> p (n t)").bitcast(I32))
-        w1_raw = [keep.tile([P, 2, H], F32, name=f"w1_raw{g}") for g in range(2)]
+        w1_raw = [keep.tile([P, 2, H], F32, name=f"w1_raw{g}", align_bytes=64) for g in range(2)]
         for g in range(2):
             nc.sync.dma_start(out=w1_raw[g][:], in_=rows(w1)[:, 2 * g : 2 * g + 2, :])
         nc.sync.dma_start(p1_sb[:], p1)
@@ -125,8 +126,9 @@ def tile_picked_ngcf8_none_p_kernel(tc, x_words, x_scales, w1, w2, w3, w4, offs,
         cast_dealt(nc.scalar.copy, "w1", w1_raw[1], 1)
         quantize_w1(2 * P, 4 * P)
 
-        w_raw["w4"] = keep.tile([P, PACK, H], F32, name="w1_bf", align_bytes=64)
-        nc.sync.dma_start(out=w_raw["w4"][:], in_=rows(w4))
+        w4_raw = [keep.tile([P, PACK, HALF], F32, name=name, align_bytes=64) for name in ("w1_bf", "w1_raw1")]
+        for g in range(2):
+            nc.sync.dma_start(out=w4_raw[g][:], in_=rows(w4)[:, :, g * HALF : (g + 1) * HALF])
 
         y_win = [keep.tile([P, WINDOW], F32, name=f"y_win{t}") for t in range(PACK)]
         pieces = [(0, 0, HALF), (0, HALF, SUB), (0, HALF + SUB, SUB)] + [(t, 0, S) for t in range(1, PACK)]
@@ -137,13 +139,20 @@ def tile_picked_ngcf8_none_p_kernel(tc, x_words, x_scales, w1, w2, w3, w4, offs,
             copy = nc.vector.tensor_copy if index == 0 else nc.scalar.copy
             copy(out=y_win[t][:, cols], in_=acc[:])
 
-        w_bf["w2"] = keep.tile([P, PACK * H], BF16, name="w1_codes", align_bytes=64)
+        w_bf["w2"] = keep.tile([P, PACK * H], BF16, name="w2_bf", align_bytes=64)
         for g in range(2):
-            nc.scalar.copy(out=w_bf["w2"][:].rearrange("p (t m j) -> p m j t", t=PACK, j=PACK)[:, g * P // 2 : (g + 1) * P // 2],
-                           in_=w2_raw[g].rearrange("p j (m t) -> p m j t", t=PACK))
-        for n in ("w3", "w4"):
-            nc.scalar.copy(out=w_bf[n][:].rearrange("p (c i j) -> p c j i", i=4, j=PACK),
-                           in_=w_raw[n][:].rearrange("p j (c i) -> p c j i", i=4))
+            nc.gpsimd.tensor_copy(out=w_bf["w2"][:].rearrange("p (t m j) -> p t m j", t=PACK, j=PACK)[:, :, g * P // 2 : (g + 1) * P // 2],
+                                  in_=w2_raw[g].rearrange("p j (m t) -> p t m j", t=PACK))
+        h1 = [keep.tile([P, S], F32, name=f"h1_{t}") for t in range(PACK)]
+        for t in range(2, PACK):
+            nc.scalar.activation(h1[t][:], y_win[t][:].indirect(p1_sb[:]), COPY)
+
+        def cast_in_place(copy, n, c0, c1, raw):
+            copy(out=w_bf[n][:, PACK * c0 : PACK * c1].rearrange("p (c i j) -> p c j i", i=4, j=PACK),
+                 in_=raw[:].rearrange("p j (c i) -> p c j i", i=4))
+
+        cast_in_place(nc.scalar.copy, "w3", 0, H, w_raw["w3"])
+        cast_in_place(nc.scalar.copy, "w4", 0, HALF, w4_raw[0])
 
         turned = [[bank(TURN_BANKS[h][b], [P, 2, 2, SUB]) for b in range(2)] for h in range(2)]
 
@@ -166,8 +175,7 @@ def tile_picked_ngcf8_none_p_kernel(tc, x_words, x_scales, w1, w2, w3, w4, offs,
                 mm(own[:, t, :], "w2", t, xw[:, cols], xs[:, cols], True, True)
             return own
 
-        h1 = [keep.tile([P, S], F32, name=f"h1_{t}") for t in range(PACK)]
-        for t in range(PACK):
+        for t in range(2):
             nc.vector.tensor_copy(h1[t][:], y_win[t][:].indirect(p1_sb[:]))
         hs = hs_row[:, S : 5 * S].rearrange("p (t s) -> p t s", t=PACK)
         for t in range(PACK):
@@ -187,6 +195,7 @@ def tile_picked_ngcf8_none_p_kernel(tc, x_words, x_scales, w1, w2, w3, w4, offs,
                         warm_up(IDLE_BANK)
             if t == 1:
                 warm_up(IDLE_BANK)
+        cast_in_place(nc.vector.tensor_copy, "w4", HALF, H, w4_raw[1])
         quantize_w("w3")
 
         zt_all = keep.tile([P, PACK * S], BF16, name="w1_bf", align_bytes=64)

@@ -80,11 +80,10 @@ def tile_picked_ngcf8_none_p_kernel(tc, x_words, x_scales, w1, w2, w3, w4, offs,
         nc.vector.tensor_copy(xs_apart[:], xs_all[:].indirect(offs_sb[:]))
         for r in range(4):
             nc.scalar.dma_start(out=xs[r:P:32, :].bitcast(I32), in_=xs_apart[112 + r : P : 4, :].bitcast(I32))
-        hs_row = placed("hs_row", [P, 5 * S], F32, 0)
-        w2_raw = [hs_row[:, first : first + 2 * S].rearrange("p (j c) -> p j c", j=PACK) for first in (0, 3 * S - SUB)]
+        w2_raw = [placed(f"w2_raw{g}", [P, PACK, HALF], F32, 2.5 + 4 * g)[:] for g in range(2)]
         for g in range(2):
             nc.sync.dma_start(out=w2_raw[g], in_=rows(w2)[:, :, g * HALF : (g + 1) * HALF])
-        w_raw = {"w3": placed("w3_raw", [P, PACK, H], F32, 10)}
+        w_raw = {"w3": placed("w3_raw", [P, PACK, H], F32, 10.5)}
         nc.sync.dma_start(out=w_raw["w3"][:], in_=rows(w3))
 
         ident = keep.tile([P, P], F32, name="ident")
@@ -126,9 +125,15 @@ def tile_picked_ngcf8_none_p_kernel(tc, x_words, x_scales, w1, w2, w3, w4, offs,
         cast_dealt(nc.scalar.copy, "w1", w1_raw[1], 1)
         quantize_w1(2 * P, 4 * P)
 
-        w4_raw = [keep.tile([P, PACK, HALF], F32, name=name, align_bytes=64) for name in ("w1_bf", "w1_raw1")]
-        for g in range(2):
-            nc.sync.dma_start(out=w4_raw[g][:], in_=rows(w4)[:, :, g * HALF : (g + 1) * HALF])
+        w_raw["w4"] = keep.tile([P, PACK, H], F32, name="w1_bf", align_bytes=64)
+        nc.sync.dma_start(out=w_raw["w4"][:], in_=rows(w4))
+
+        w_bf["w2"] = keep.tile([P, PACK * H], BF16, name="w2_bf", align_bytes=64)
+        h1 = [keep.tile([P, S], F32, name=f"h1_{t}") for t in range(PACK)]
+
+        def cast_w2(g):
+            nc.vector.tensor_copy(out=w_bf["w2"][:].rearrange("p (t m j) -> p m j t", t=PACK, j=PACK)[:, g * P // 2 : (g + 1) * P // 2],
+                                  in_=w2_raw[g].rearrange("p j (m t) -> p m j t", t=PACK))
 
         y_win = [keep.tile([P, WINDOW], F32, name=f"y_win{t}") for t in range(PACK)]
         pieces = [(0, 0, HALF), (0, HALF, SUB), (0, HALF + SUB, SUB)] + [(t, 0, S) for t in range(1, PACK)]
@@ -136,23 +141,18 @@ def tile_picked_ngcf8_none_p_kernel(tc, x_words, x_scales, w1, w2, w3, w4, offs,
             cols = slice(j0, j0 + width)
             acc = bank(index % Y_BANKS, [P, width])
             mm(acc[:], "w1", t, xw[:, cols], xs[:, cols], True, True)
-            copy = nc.vector.tensor_copy if index == 0 else nc.scalar.copy
+            copy = nc.vector.tensor_copy if index == 0 or t == 1 else nc.scalar.copy
             copy(out=y_win[t][:, cols], in_=acc[:])
-
-        w_bf["w2"] = keep.tile([P, PACK * H], BF16, name="w2_bf", align_bytes=64)
-        for g in range(2):
-            nc.gpsimd.tensor_copy(out=w_bf["w2"][:].rearrange("p (t m j) -> p t m j", t=PACK, j=PACK)[:, :, g * P // 2 : (g + 1) * P // 2],
-                                  in_=w2_raw[g].rearrange("p j (m t) -> p t m j", t=PACK))
-        h1 = [keep.tile([P, S], F32, name=f"h1_{t}") for t in range(PACK)]
-        for t in range(2, PACK):
-            nc.scalar.activation(h1[t][:], y_win[t][:].indirect(p1_sb[:]), COPY)
+            if t == 1:
+                cast_w2(0)
+            if j0 + width == S:
+                nc.scalar.activation(h1[t][:], y_win[t][:].indirect(p1_sb[:]), COPY)
 
         def cast_in_place(copy, n, c0, c1, raw):
             copy(out=w_bf[n][:, PACK * c0 : PACK * c1].rearrange("p (c i j) -> p c j i", i=4, j=PACK),
                  in_=raw[:].rearrange("p j (c i) -> p c j i", i=4))
 
-        cast_in_place(nc.scalar.copy, "w3", 0, H, w_raw["w3"])
-        cast_in_place(nc.scalar.copy, "w4", 0, HALF, w4_raw[0])
+        cast_in_place(nc.scalar.copy, "w4", 0, H, w_raw["w4"])
 
         turned = [[bank(TURN_BANKS[h][b], [P, 2, 2, SUB]) for b in range(2)] for h in range(2)]
 
@@ -175,14 +175,17 @@ def tile_picked_ngcf8_none_p_kernel(tc, x_words, x_scales, w1, w2, w3, w4, offs,
                 mm(own[:, t, :], "w2", t, xw[:, cols], xs[:, cols], True, True)
             return own
 
-        for t in range(2):
-            nc.vector.tensor_copy(h1[t][:], y_win[t][:].indirect(p1_sb[:]))
-        hs = hs_row[:, S : 5 * S].rearrange("p (t s) -> p t s", t=PACK)
+        hs_row = keep.tile([P, PACK * S], F32, name="hs_row")
+        hs = hs_row[:].rearrange("p (t s) -> p t s", t=PACK)
         for t in range(PACK):
             if t == 1:
+                cast_w2(1)
+            if t == 2:
                 quantize_w("w2")
                 c = {v: make_c(v) for v in range(2)}
                 warm_up(IDLE_BANK)
+            if t == 3:
+                cast_in_place(nc.vector.tensor_copy, "w3", 0, H, w_raw["w3"])
             if t < PACK - 1:
                 nc.vector.tensor_tensor(hs[:, t, :], y_win[t][:].indirect(p2_sb[:]), h1[t][:], ADD)
                 turn(hs[:, t, :], t, False)
@@ -193,9 +196,8 @@ def tile_picked_ngcf8_none_p_kernel(tc, x_words, x_scales, w1, w2, w3, w4, offs,
                     turn(hs[:, t, :], t, False, range(2 * b, 2 * b + 2))
                     if b == 0:
                         warm_up(IDLE_BANK)
-            if t == 1:
+            if t == 2:
                 warm_up(IDLE_BANK)
-        cast_in_place(nc.vector.tensor_copy, "w4", HALF, H, w4_raw[1])
         quantize_w("w3")
 
         zt_all = keep.tile([P, PACK * S], BF16, name="w1_bf", align_bytes=64)

@@ -31,7 +31,6 @@ TURN_BANKS = ((4, 5), (6, 7))
 C_BANKS = (0, 1, 4, 7)
 BACK_BANKS = (4, 5)
 OUT_BANKS = ((0, 1, 3, 2), (6, 4), (0, 1, 5, 3))
-IDLE_BANK = 2
 KIB = 1024
 
 
@@ -183,9 +182,6 @@ def tile_picked_ngcf8_none_p_kernel(tc, x_words, x_scales, w1, w2, w3, w4, offs,
             if t == 2:
                 quantize_w("w2")
                 c = {v: make_c(v) for v in range(2)}
-                warm_up(IDLE_BANK)
-            if t == 3:
-                cast_in_place(nc.vector.tensor_copy, "w3", 0, H, w_raw["w3"])
             if t < PACK - 1:
                 nc.vector.tensor_tensor(hs[:, t, :], y_win[t][:].indirect(p2_sb[:]), h1[t][:], ADD)
                 turn(hs[:, t, :], t, False)
@@ -194,11 +190,7 @@ def tile_picked_ngcf8_none_p_kernel(tc, x_words, x_scales, w1, w2, w3, w4, offs,
                     cols = slice(b * HALF, (b + 1) * HALF)
                     nc.vector.tensor_tensor(hs[:, t, cols], y_win[t][:].indirect(p2_sb[:, list_columns(b * HALF, HALF)]), h1[t][:, cols], ADD)
                     turn(hs[:, t, :], t, False, range(2 * b, 2 * b + 2))
-                    if b == 0:
-                        warm_up(IDLE_BANK)
-            if t == 2:
-                warm_up(IDLE_BANK)
-        quantize_w("w3")
+        cast_in_place(nc.vector.tensor_copy, "w3", 0, H, w_raw["w3"])
 
         zt_all = keep.tile([P, PACK * S], BF16, name="w1_bf", align_bytes=64)
         wide = HALF * PACK
@@ -243,6 +235,7 @@ def tile_picked_ngcf8_none_p_kernel(tc, x_words, x_scales, w1, w2, w3, w4, offs,
         res = keep.tile([P, PACK, S], F32, name="res")
         product(0, both[:, wide : wide + SUB * PACK])
         product(1, both[:, wide + SUB * PACK : 2 * wide])
+        quantize_w("w3")
         quantize_w("w4")
         turn_back(0, 0)
         turn_back(0, 1)

@@ -28,9 +28,9 @@ WINDOW = 2 * S
 
 Y_BANKS = 4
 TURN_BANKS = ((4, 5), (6, 7))
-C_BANKS = (0, 1, 4, 7)
+C_BANKS = (0, 1, 6, 4)
 BACK_BANKS = (4, 5)
-OUT_BANKS = ((0, 1, 3, 2), (6, 4), (0, 1, 5, 3))
+OUT_BANKS = ((0, 1, 3, 2), (7, 6), (0, 1, 5, 3))
 KIB = 1024
 
 
@@ -88,8 +88,10 @@ def tile_picked_ngcf8_none_p_kernel(tc, x_words, x_scales, w1, w2, w3, w4, offs,
         ident = keep.tile([P, P], F32, name="ident")
         make_identity(nc, ident[:])
         names = ("w1", "w2", "w3", "w4")
-        w_bf = {n: keep.tile([P, PACK * H], BF16, name=f"{n}_bf", align_bytes=64) for n in names if n != "w2"}
-        w_codes = {n: keep.tile([P, H], U32, name=f"{n}_codes", align_bytes=64) for n in names}
+        w_bf = {n: keep.tile([P, PACK * H], BF16, name=f"{n}_bf", align_bytes=64) for n in ("w4",)}
+        w_bf["w3"] = placed("w3_bf", [P, PACK * H], BF16, 40)
+        w_bf["w1"] = placed("w1_bf", [P, PACK * H], BF16, 20)
+        w_codes = {n: keep.tile([P, H], U32, name=f"{n}_codes", align_bytes=64) for n in ("w1", "w2", "w4")}
         w_scale = {n: keep.tile([P, H], U8, name=f"{n}_scale", align_bytes=64) for n in names}
 
         def cast_tile(copy, t, m0, m1):
@@ -124,7 +126,7 @@ def tile_picked_ngcf8_none_p_kernel(tc, x_words, x_scales, w1, w2, w3, w4, offs,
         cast_dealt(nc.scalar.copy, "w1", w1_raw[1], 1)
         quantize_w1(2 * P, 4 * P)
 
-        w_raw["w4"] = keep.tile([P, PACK, H], F32, name="w1_bf", align_bytes=64)
+        w_raw["w4"] = placed("w4_raw", [P, PACK, H], F32, 20)
         nc.sync.dma_start(out=w_raw["w4"][:], in_=rows(w4))
 
         w_bf["w2"] = keep.tile([P, PACK * H], BF16, name="w2_bf", align_bytes=64)
@@ -164,9 +166,6 @@ def tile_picked_ngcf8_none_p_kernel(tc, x_words, x_scales, w1, w2, w3, w4, offs,
         for t in range(PACK):
             turn(y_win[t], t, True)
 
-        def warm_up(index):
-            mm(bank(index, [P, S])[:], "w2", 0, xw[:], xs[:], True, True)
-
         def make_c(v):
             cols = slice(v * SUB, (v + 1) * SUB)
             own = bank(C_BANKS[v], [P, PACK, SUB])
@@ -192,15 +191,14 @@ def tile_picked_ngcf8_none_p_kernel(tc, x_words, x_scales, w1, w2, w3, w4, offs,
                     turn(hs[:, t, :], t, False, range(2 * b, 2 * b + 2))
         cast_in_place(nc.vector.tensor_copy, "w3", 0, H, w_raw["w3"])
 
-        zt_all = keep.tile([P, PACK * S], BF16, name="w1_bf", align_bytes=64)
         wide = HALF * PACK
-        both = placed("both", [P, 2 * wide], BF16, 12)
-        z_in = [both[:, 0:wide], keep.tile([P, wide], BF16, name="z_in1", align_bytes=64)[:]]
+        z2_first = placed("z2_first", [P, wide], BF16, 12)
+        z_in = [placed(f"z_in{b}", [P, wide], BF16, 34 + 2 * b)[:] for b in range(2)]
         out_rows = out.rearrange("(a p) j -> p a j", p=P)
 
         def product(v, dst):
             cols = slice(v * SUB, (v + 1) * SUB)
-            own = c[v] if v in c else make_c(v)
+            own = c[v]
             nc.vector.tensor_tensor(
                 dst.rearrange("p (c i t) -> p c t i", i=2, t=PACK),
                 own[:].rearrange("p t (c i) -> p c t i", i=2),
@@ -213,46 +211,47 @@ def tile_picked_ngcf8_none_p_kernel(tc, x_words, x_scales, w1, w2, w3, w4, offs,
         def turn_back(h, b):
             if h == 0:
                 back[b] = bank(BACK_BANKS[b], [P, 2, 2, SUB])
-            first = (2 * h + b) * 4 * SUB
-            zt_bf = zt_all[:, first : first + 4 * SUB]
+            zt_bf = placed(f"zt{h}{b}", [P, 4 * SUB], BF16, (20, 21, 24, 27)[2 * h + b])[:]
             nc.scalar.copy(out=zt_bf.rearrange("k (u p e) -> k u p e", u=2, e=2), in_=turned[h][b][:].rearrange("k u e p -> k u p e"))
             for u in range(2):
                 nc.tensor.transpose(back[b][:, u, h, :], zt_bf.bitcast(F32)[:, u * P : (u + 1) * P], ident[:])
             if h == 1:
                 if b == 0:
-                    warm_up(TURN_BANKS[h][b])
-                else:
-                    c[3] = make_c(3)
+                    c[2] = make_c(2)
                 nc.scalar.copy(out=z_in[b].bitcast(F32).rearrange("p (u k h) -> p u k h", u=2, h=2), in_=back[b][:].rearrange("p u h k -> p u k h"))
 
-        def quantize_z(name, src):
+        def quantize_z(name, src, kib):
             width = src.shape[1] // PACK
-            codes = keep.tile([P, width], U32, name=f"{name}_codes", align_bytes=64)
+            codes = placed(f"{name}_codes", [P, width], U32, kib)
             scale = keep.tile([P, width], U8, name=f"{name}_scale", align_bytes=64)
             nc.vector.quantize_mx(out=codes[:].bitcast(FP8X4), scales=scale[:], in_=src)
             return codes, scale
 
         res = keep.tile([P, PACK, S], F32, name="res")
-        product(0, both[:, wide : wide + SUB * PACK])
-        product(1, both[:, wide + SUB * PACK : 2 * wide])
-        quantize_w("w3")
+        product(0, z2_first[:, 0 : SUB * PACK])
+        product(1, z2_first[:, SUB * PACK : wide])
         quantize_w("w4")
         turn_back(0, 0)
         turn_back(0, 1)
         turn_back(1, 0)
-        codes, scale = quantize_z("first", both[:])
         turn_back(1, 1)
-        z2_third = keep.tile([P, SUB * PACK], BF16, name="z2_third", align_bytes=64)
+        z2c, z2s = quantize_z("early", z2_first[:], 23.5)
+        accs = [bank(index, [P, HALF]) for index in OUT_BANKS[0]]
+        for a in range(PACK):
+            mm(accs[a][:], "w4", a, z2c[:], z2s[:], True, False)
+        w_codes["w3"] = placed("w3_codes", [P, H], U32, 24.5)
+        quantize_w("w3")
+        codes, scale = quantize_z("first", z_in[0], 30)
+        c[3] = make_c(3)
+        z2_third = placed("z2_third", [P, SUB * PACK], BF16, 40)
         product(2, z2_third[:])
         for a in range(PACK):
-            acc = bank(OUT_BANKS[0][a], [P, HALF])
-            for which, n in enumerate(("w3", "w4")):
-                cols = slice(which * HALF, (which + 1) * HALF)
-                mm(acc[:], n, a, codes[:, cols], scale[:, cols], which == 0, which == 1)
+            acc = accs[a]
+            mm(acc[:], "w3", a, codes[:], scale[:], False, True)
             nc.scalar.copy(out=res[:, a, 0:HALF], in_=acc[:])
             nc.sync.dma_start(out=out_rows[:, a, 0:HALF], in_=res[:, a, 0:HALF])
-        zc, zs = quantize_z("second", z_in[1])
-        z2c, z2s = quantize_z("third", z2_third[:])
+        zc, zs = quantize_z("second", z_in[1], 31)
+        z2c, z2s = quantize_z("third", z2_third[:], 32)
         third = slice(HALF, HALF + SUB)
         for g in range(2):
             acc = bank(OUT_BANKS[1][g], [P, 2, SUB])
@@ -261,12 +260,12 @@ def tile_picked_ngcf8_none_p_kernel(tc, x_words, x_scales, w1, w2, w3, w4, offs,
                 mm(acc[:, a, :], "w4", 2 * g + a, z2c[:], z2s[:], False, True)
             nc.scalar.copy(out=res[:, 2 * g : 2 * g + 2, third], in_=acc[:])
             nc.sync.dma_start(out=out_rows[:, 2 * g : 2 * g + 2, third], in_=res[:, 2 * g : 2 * g + 2, third])
-        z2_last = keep.tile([P, SUB * PACK], BF16, name="w1_bf", align_bytes=64)
+        z2_last = placed("z2_last", [P, SUB * PACK], BF16, 35)
         product(3, z2_last[:])
         accs = [bank(index, [P, SUB]) for index in OUT_BANKS[2]]
         for a in range(PACK):
             mm(accs[a][:], "w3", a, zc[:, SUB:HALF], zs[:, SUB:HALF], True, False)
-        z2c, z2s = quantize_z("last", z2_last[:])
+        z2c, z2s = quantize_z("last", z2_last[:], 33)
         last = slice(HALF + SUB, S)
         for a in range(PACK):
             mm(accs[a][:], "w4", a, z2c[:], z2s[:], False, True)

@@ -28,9 +28,9 @@ WINDOW = 2 * S
 
 Y_BANKS = 4
 TURN_BANKS = ((4, 5), (6, 7))
-C_BANKS = (0, 1, 6, 4)
-BACK_BANKS = (4, 5)
-OUT_BANKS = ((0, 1, 3, 2), (7, 6), (0, 1, 5, 3))
+C_BANKS = (0, 1, 4, 5)
+BACK_BANKS = (2, 3)
+OUT_BANKS = ((0, 1, 6, 7), (2, 4), (0, 1, 3, 6))
 KIB = 1024
 
 
@@ -43,9 +43,6 @@ def tile_picked_ngcf8_none_p_kernel(tc, x_words, x_scales, w1, w2, w3, w4, offs,
 
         def bank(index, shape):
             return psum.tile(shape, F32, name=f"bank{index}")
-
-        def list_columns(j0, width):
-            return slice(j0 // 16, (j0 + width) // 16)
 
         def placed(name, shape, dtype, kib):
             return shared.tile(shape, dtype, name=name, offset=int(kib * KIB), align_bytes=64)
@@ -157,8 +154,8 @@ def tile_picked_ngcf8_none_p_kernel(tc, x_words, x_scales, w1, w2, w3, w4, offs,
 
         turned = [[bank(TURN_BANKS[h][b], [P, 2, 2, SUB]) for b in range(2)] for h in range(2)]
 
-        def turn(src, t, first, runs=range(RUNS)):
-            for v in runs:
+        def turn(src, t, first):
+            for v in range(RUNS):
                 edge = v % 2 == t % 2
                 nc.tensor.matmul(turned[t // 2][v // 2][:, v % 2, t % 2, :], lhsT=src[:, v * SUB : (v + 1) * SUB], rhs=ident[:], is_transpose=True,
                                  start=first and edge and t % 2 == 0, stop=not first and edge and t % 2 == 1)
@@ -181,14 +178,8 @@ def tile_picked_ngcf8_none_p_kernel(tc, x_words, x_scales, w1, w2, w3, w4, offs,
             if t == 2:
                 quantize_w("w2")
                 c = {v: make_c(v) for v in range(2)}
-            if t < PACK - 1:
-                nc.vector.tensor_tensor(hs[:, t, :], y_win[t][:].indirect(p2_sb[:]), h1[t][:], ADD)
-                turn(hs[:, t, :], t, False)
-            else:
-                for b in range(2):
-                    cols = slice(b * HALF, (b + 1) * HALF)
-                    nc.vector.tensor_tensor(hs[:, t, cols], y_win[t][:].indirect(p2_sb[:, list_columns(b * HALF, HALF)]), h1[t][:, cols], ADD)
-                    turn(hs[:, t, :], t, False, range(2 * b, 2 * b + 2))
+            nc.vector.tensor_tensor(hs[:, t, :], y_win[t][:].indirect(p2_sb[:]), h1[t][:], ADD)
+            turn(hs[:, t, :], t, False)
         cast_in_place(nc.vector.tensor_copy, "w3", 0, H, w_raw["w3"])
 
         wide = HALF * PACK
@@ -215,9 +206,11 @@ def tile_picked_ngcf8_none_p_kernel(tc, x_words, x_scales, w1, w2, w3, w4, offs,
             nc.scalar.copy(out=zt_bf.rearrange("k (u p e) -> k u p e", u=2, e=2), in_=turned[h][b][:].rearrange("k u e p -> k u p e"))
             for u in range(2):
                 nc.tensor.transpose(back[b][:, u, h, :], zt_bf.bitcast(F32)[:, u * P : (u + 1) * P], ident[:])
+            if h == 0:
+                c[2 + b] = make_c(2 + b)
             if h == 1:
-                if b == 0:
-                    c[2] = make_c(2)
+                width = (S, HALF)[b]
+                mm(bank(TURN_BANKS[h][b], [P, width])[:], "w2", 0, xw[:, 0:width], xs[:, 0:width], True, True)
                 nc.scalar.copy(out=z_in[b].bitcast(F32).rearrange("p (u k h) -> p u k h", u=2, h=2), in_=back[b][:].rearrange("p u h k -> p u k h"))
 
         def quantize_z(name, src, kib):
@@ -242,7 +235,6 @@ def tile_picked_ngcf8_none_p_kernel(tc, x_words, x_scales, w1, w2, w3, w4, offs,
         w_codes["w3"] = placed("w3_codes", [P, H], U32, 24.5)
         quantize_w("w3")
         codes, scale = quantize_z("first", z_in[0], 30)
-        c[3] = make_c(3)
         z2_third = placed("z2_third", [P, SUB * PACK], BF16, 40)
         product(2, z2_third[:])
         for a in range(PACK):

@@ -28,10 +28,11 @@ WINDOW = 2 * S
 
 Y_BANKS = 4
 TURN_BANKS = ((4, 5), (6, 7))
-C_BANKS = (0, 1, 4, 5)
-BACK_BANKS = (2, 3)
-OUT_BANKS = ((0, 1, 6, 7), (2, 4), (0, 1, 3, 6))
+C_BANKS = (0, 1, 2, 4)
+BACK_BANKS = (3, 0)
+OUT_BANKS = ((1, 2, 5, 6), (3, 7), (0, 1, 2, 5))
 KIB = 1024
+W3_SPLIT = 256
 
 
 def tile_picked_ngcf8_none_p_kernel(tc, x_words, x_scales, w1, w2, w3, w4, offs, p1, p2, out):
@@ -79,15 +80,16 @@ def tile_picked_ngcf8_none_p_kernel(tc, x_words, x_scales, w1, w2, w3, w4, offs,
         w2_raw = [placed(f"w2_raw{g}", [P, PACK, HALF], F32, 2.5 + 4 * g)[:] for g in range(2)]
         for g in range(2):
             nc.sync.dma_start(out=w2_raw[g], in_=rows(w2)[:, :, g * HALF : (g + 1) * HALF])
-        w_raw = {"w3": placed("w3_raw", [P, PACK, H], F32, 10.5)}
-        nc.sync.dma_start(out=w_raw["w3"][:], in_=rows(w3))
+        w3_row = placed("w3_row", [P, 2 * H - SUB + PACK * W3_SPLIT], F32, 10.5)
+        w_raw = {"w3": w3_row[:, 2 * H - SUB :].rearrange("p (j c) -> p j c", j=PACK)}
+        nc.sync.dma_start(out=w_raw["w3"], in_=rows(w3)[:, :, 0:W3_SPLIT])
 
         ident = keep.tile([P, P], F32, name="ident")
         make_identity(nc, ident[:])
         names = ("w1", "w2", "w3", "w4")
         w_bf = {n: keep.tile([P, PACK * H], BF16, name=f"{n}_bf", align_bytes=64) for n in ("w4",)}
-        w_bf["w3"] = placed("w3_bf", [P, PACK * H], BF16, 40)
-        w_bf["w1"] = placed("w1_bf", [P, PACK * H], BF16, 20)
+        w_bf["w3"] = w3_row[:, 0 : 2 * H].bitcast(BF16)
+        w_bf["w1"] = placed("w1_bf", [P, PACK * H], BF16, 44)
         w_codes = {n: keep.tile([P, H], U32, name=f"{n}_codes", align_bytes=64) for n in ("w1", "w2", "w4")}
         w_scale = {n: keep.tile([P, H], U8, name=f"{n}_scale", align_bytes=64) for n in names}
 
@@ -123,7 +125,9 @@ def tile_picked_ngcf8_none_p_kernel(tc, x_words, x_scales, w1, w2, w3, w4, offs,
         cast_dealt(nc.scalar.copy, "w1", w1_raw[1], 1)
         quantize_w1(2 * P, 4 * P)
 
-        w_raw["w4"] = placed("w4_raw", [P, PACK, H], F32, 20)
+        w3_rest = keep.tile([P, PACK, H - W3_SPLIT], F32, name="w1_raw1", align_bytes=64)
+        nc.sync.dma_start(out=w3_rest[:], in_=rows(w3)[:, :, W3_SPLIT:H])
+        w_raw["w4"] = placed("w4_raw", [P, PACK, H], F32, 44)
         nc.sync.dma_start(out=w_raw["w4"][:], in_=rows(w4))
 
         w_bf["w2"] = keep.tile([P, PACK * H], BF16, name="w2_bf", align_bytes=64)
@@ -148,7 +152,7 @@ def tile_picked_ngcf8_none_p_kernel(tc, x_words, x_scales, w1, w2, w3, w4, offs,
 
         def cast_in_place(copy, n, c0, c1, raw):
             copy(out=w_bf[n][:, PACK * c0 : PACK * c1].rearrange("p (c i j) -> p c j i", i=4, j=PACK),
-                 in_=raw[:].rearrange("p j (c i) -> p c j i", i=4))
+                 in_=raw[:, :, c0:c1].rearrange("p j (c i) -> p c j i", i=4))
 
         cast_in_place(nc.scalar.copy, "w4", 0, H, w_raw["w4"])
 
@@ -177,13 +181,15 @@ def tile_picked_ngcf8_none_p_kernel(tc, x_words, x_scales, w1, w2, w3, w4, offs,
                 cast_w2(1)
             if t == 2:
                 quantize_w("w2")
-                c = {v: make_c(v) for v in range(2)}
+                c = {v: make_c(v) for v in range(3)}
             nc.vector.tensor_tensor(hs[:, t, :], y_win[t][:].indirect(p2_sb[:]), h1[t][:], ADD)
             turn(hs[:, t, :], t, False)
-        cast_in_place(nc.vector.tensor_copy, "w3", 0, H, w_raw["w3"])
+        cast_in_place(nc.vector.tensor_copy, "w3", 0, W3_SPLIT, w_raw["w3"])
+        nc.gpsimd.tensor_copy(out=w_bf["w3"][:, PACK * W3_SPLIT : PACK * H].rearrange("p (c j) -> p c j", j=PACK),
+                              in_=w3_rest[:].rearrange("p j c -> p c j"))
 
         wide = HALF * PACK
-        z2_first = placed("z2_first", [P, wide], BF16, 12)
+        z2_first = w3_row[:, 2 * H : 2 * H + wide // 2].bitcast(BF16)
         z_in = [placed(f"z_in{b}", [P, wide], BF16, 34 + 2 * b)[:] for b in range(2)]
         out_rows = out.rearrange("(a p) j -> p a j", p=P)
 
@@ -202,15 +208,16 @@ def tile_picked_ngcf8_none_p_kernel(tc, x_words, x_scales, w1, w2, w3, w4, offs,
         def turn_back(h, b):
             if h == 0:
                 back[b] = bank(BACK_BANKS[b], [P, 2, 2, SUB])
-            zt_bf = placed(f"zt{h}{b}", [P, 4 * SUB], BF16, (20, 21, 24, 27)[2 * h + b])[:]
+            zt_bf = placed(f"zt{h}{b}", [P, 4 * SUB], BF16, (44, 45, 48, 51)[2 * h + b])[:]
             nc.scalar.copy(out=zt_bf.rearrange("k (u p e) -> k u p e", u=2, e=2), in_=turned[h][b][:].rearrange("k u e p -> k u p e"))
             for u in range(2):
                 nc.tensor.transpose(back[b][:, u, h, :], zt_bf.bitcast(F32)[:, u * P : (u + 1) * P], ident[:])
-            if h == 0:
-                c[2 + b] = make_c(2 + b)
-            if h == 1:
-                width = (S, HALF)[b]
+            if (h, b) == (0, 0):
+                c[3] = make_c(3)
+            elif (h, b) != (1, 1):
+                width = (S, HALF)[h]
                 mm(bank(TURN_BANKS[h][b], [P, width])[:], "w2", 0, xw[:, 0:width], xs[:, 0:width], True, True)
+            if h == 1:
                 nc.scalar.copy(out=z_in[b].bitcast(F32).rearrange("p (u k h) -> p u k h", u=2, h=2), in_=back[b][:].rearrange("p u h k -> p u k h"))
 
         def quantize_z(name, src, kib):
@@ -223,34 +230,35 @@ def tile_picked_ngcf8_none_p_kernel(tc, x_words, x_scales, w1, w2, w3, w4, offs,
         res = keep.tile([P, PACK, S], F32, name="res")
         product(0, z2_first[:, 0 : SUB * PACK])
         product(1, z2_first[:, SUB * PACK : wide])
+        z2_third = w3_row[:, 2 * H + wide // 2 : 2 * H + 3 * wide // 4].bitcast(BF16)
+        product(2, z2_third)
         quantize_w("w4")
         turn_back(0, 0)
         turn_back(0, 1)
         turn_back(1, 0)
         turn_back(1, 1)
-        z2c, z2s = quantize_z("early", z2_first[:], 23.5)
+        z2c, z2s = quantize_z("early", z2_first, 47.5)
         accs = [bank(index, [P, HALF]) for index in OUT_BANKS[0]]
         for a in range(PACK):
             mm(accs[a][:], "w4", a, z2c[:], z2s[:], True, False)
-        w_codes["w3"] = placed("w3_codes", [P, H], U32, 24.5)
+        w_codes["w3"] = placed("w3_codes", [P, H], U32, 48.5)
         quantize_w("w3")
         codes, scale = quantize_z("first", z_in[0], 30)
-        z2_third = placed("z2_third", [P, SUB * PACK], BF16, 40)
-        product(2, z2_third[:])
         for a in range(PACK):
             acc = accs[a]
             mm(acc[:], "w3", a, codes[:], scale[:], False, True)
             nc.scalar.copy(out=res[:, a, 0:HALF], in_=acc[:])
             nc.sync.dma_start(out=out_rows[:, a, 0:HALF], in_=res[:, a, 0:HALF])
         zc, zs = quantize_z("second", z_in[1], 31)
-        z2c, z2s = quantize_z("third", z2_third[:], 32)
+        z2c, z2s = quantize_z("third", z2_third, 34.5)
         third = slice(HALF, HALF + SUB)
         for g in range(2):
             acc = bank(OUT_BANKS[1][g], [P, 2, SUB])
             for a in range(2):
                 mm(acc[:, a, :], "w3", 2 * g + a, zc[:, 0:SUB], zs[:, 0:SUB], True, False)
                 mm(acc[:, a, :], "w4", 2 * g + a, z2c[:], z2s[:], False, True)
-            nc.scalar.copy(out=res[:, 2 * g : 2 * g + 2, third], in_=acc[:])
+            copy = nc.scalar.copy if g == 0 else nc.vector.tensor_copy
+            copy(out=res[:, 2 * g : 2 * g + 2, third], in_=acc[:])
             nc.sync.dma_start(out=out_rows[:, 2 * g : 2 * g + 2, third], in_=res[:, 2 * g : 2 * g + 2, third])
         z2_last = placed("z2_last", [P, SUB * PACK], BF16, 35)
         product(3, z2_last[:])

@@ -28,9 +28,9 @@ WINDOW = 2 * S
 
 Y_BANKS = 4
 TURN_BANKS = ((4, 5), (6, 7))
-C_BANKS = (0, 1, 2, 4)
-BACK_BANKS = (3, 0)
-OUT_BANKS = ((1, 2, 5, 6), (3, 7), (0, 1, 2, 5))
+C_BANKS = (0, 1, 4, 5)
+BACK_BANKS = (2, 3)
+OUT_BANKS = ((0, 1, 6, 7), (2, 4), (3, 5, 0, 1))
 KIB = 1024
 W3_SPLIT = 256
 
@@ -90,7 +90,7 @@ def tile_picked_ngcf8_none_p_kernel(tc, x_words, x_scales, w1, w2, w3, w4, offs,
         w_bf = {n: keep.tile([P, PACK * H], BF16, name=f"{n}_bf", align_bytes=64) for n in ("w4",)}
         w_bf["w3"] = w3_row[:, 0 : 2 * H].bitcast(BF16)
         w_bf["w1"] = placed("w1_bf", [P, PACK * H], BF16, 44)
-        w_codes = {n: keep.tile([P, H], U32, name=f"{n}_codes", align_bytes=64) for n in ("w1", "w2", "w4")}
+        w_codes = {n: keep.tile([P, H], U32, name=f"{n}_codes", align_bytes=64) for n in ("w1", "w2")}
         w_scale = {n: keep.tile([P, H], U8, name=f"{n}_scale", align_bytes=64) for n in names}
 
         def cast_tile(copy, t, m0, m1):
@@ -181,7 +181,7 @@ def tile_picked_ngcf8_none_p_kernel(tc, x_words, x_scales, w1, w2, w3, w4, offs,
                 cast_w2(1)
             if t == 2:
                 quantize_w("w2")
-                c = {v: make_c(v) for v in range(3)}
+                c = {v: make_c(v) for v in range(2)}
             nc.vector.tensor_tensor(hs[:, t, :], y_win[t][:].indirect(p2_sb[:]), h1[t][:], ADD)
             turn(hs[:, t, :], t, False)
         cast_in_place(nc.vector.tensor_copy, "w3", 0, W3_SPLIT, w_raw["w3"])
@@ -210,14 +210,15 @@ def tile_picked_ngcf8_none_p_kernel(tc, x_words, x_scales, w1, w2, w3, w4, offs,
                 back[b] = bank(BACK_BANKS[b], [P, 2, 2, SUB])
             zt_bf = placed(f"zt{h}{b}", [P, 4 * SUB], BF16, (44, 45, 48, 51)[2 * h + b])[:]
             nc.scalar.copy(out=zt_bf.rearrange("k (u p e) -> k u p e", u=2, e=2), in_=turned[h][b][:].rearrange("k u e p -> k u p e"))
+            if (h, b) == (0, 0):
+                c[2] = make_c(2)
             for u in range(2):
                 nc.tensor.transpose(back[b][:, u, h, :], zt_bf.bitcast(F32)[:, u * P : (u + 1) * P], ident[:])
-            if (h, b) == (0, 0):
+            if (h, b) == (0, 1):
                 c[3] = make_c(3)
-            elif (h, b) != (1, 1):
-                width = (S, HALF)[h]
-                mm(bank(TURN_BANKS[h][b], [P, width])[:], "w2", 0, xw[:, 0:width], xs[:, 0:width], True, True)
             if h == 1:
+                width = (S, HALF)[b]
+                mm(bank(TURN_BANKS[h][b], [P, width])[:], "w2", 0, xw[:, 0:width], xs[:, 0:width], True, True)
                 nc.scalar.copy(out=z_in[b].bitcast(F32).rearrange("p (u k h) -> p u k h", u=2, h=2), in_=back[b][:].rearrange("p u h k -> p u k h"))
 
         def quantize_z(name, src, kib):
@@ -230,10 +231,11 @@ def tile_picked_ngcf8_none_p_kernel(tc, x_words, x_scales, w1, w2, w3, w4, offs,
         res = keep.tile([P, PACK, S], F32, name="res")
         product(0, z2_first[:, 0 : SUB * PACK])
         product(1, z2_first[:, SUB * PACK : wide])
+        turn_back(0, 0)
         z2_third = w3_row[:, 2 * H + wide // 2 : 2 * H + 3 * wide // 4].bitcast(BF16)
         product(2, z2_third)
+        w_codes["w4"] = placed("w4_codes", [P, H], U32, 42.5)
         quantize_w("w4")
-        turn_back(0, 0)
         turn_back(0, 1)
         turn_back(1, 0)
         turn_back(1, 1)

from contextlib import ExitStack

import concourse.mybir as mybir
from concourse.masks import make_identity

T, S, H = 2048, 512, 512
FLOPS = 4 * 2 * 512 * 512 * 512

F32 = mybir.dt.float32
BF16 = mybir.dt.bfloat16
I32 = mybir.dt.int32
U32 = mybir.dt.uint32
U16 = mybir.dt.uint16
U8 = mybir.dt.uint8
FP8X4 = mybir.dt.float8_e4m3fn_x4
ADD = mybir.AluOpType.add
MULT = mybir.AluOpType.mult
COPY = mybir.ActivationFunctionType.Copy

P = 128
PACK = 4
SUB = 128
HALF = S // 2
RUNS = S // SUB
SHARE = 84
EARLY_SHARE = 64
WINDOW = 2 * S

Y_BANKS = 4
TURN_BANKS = ((4, 5), (6, 7))
C_BANKS = (0, 1, 4, 5)
BACK_BANKS = (2, 3)
OUT_BANKS = ((0, 1, 6, 7), (2, 4), (3, 5, 0, 1))
KIB = 1024
W3_SPLIT = 256


def tile_picked_ngcf8_none_p_kernel(tc, x_words, x_scales, w1, w2, w3, w4, offs, p1, p2, out):
    nc = tc.nc
    with ExitStack() as ctx:
        keep = ctx.enter_context(tc.tile_pool(name="keep", bufs=1))
        shared = ctx.enter_context(tc.tile_pool(name="shared", bufs=1))
        psum = ctx.enter_context(tc.psum_pool(name="psum", bufs=1))

        def bank(index, shape):
            return psum.tile(shape, F32, name=f"bank{index}")

        def placed(name, shape, dtype, kib):
            return shared.tile(shape, dtype, name=name, offset=int(kib * KIB), align_bytes=64)

        def rows(w):
            return w.rearrange("(p j) c -> p j c", j=PACK)

        offs_sb = keep.tile([P, S // 16], U16, name="offs_sb")
        p1_sb = keep.tile([P, S // 16], U16, name="p1_sb")
        p2_sb = keep.tile([P, S // 16], U16, name="p2_sb")
        xw_all = placed("xw_all", [P, T], I32, 6)
        xs_all = keep.tile([P, T], U8, name="xs_all", align_bytes=64)
        xw = keep.tile([P, S], U32, name="xw", align_bytes=64)
        xs_apart = keep.tile([P, S], U8, name="xs_apart", align_bytes=64)
        xs = keep.tile([P, S], U8, name="xs", align_bytes=64)

        nc.gpsimd.memset(xs_all[96:112, :].bitcast(I32), 0)
        nc.vector.memset(xs_all[0:96, :].bitcast(I32), 0)
        nc.gpsimd.memset(xs[:].bitcast(I32), 0)
        nc.scalar.dma_start(out=xs_all[112:P, :].bitcast(I32), in_=x_scales[0].bitcast(I32))
        early = keep.tile([P, 2], F32, name="early")
        nc.gpsimd.memset(early[:, 0:1], 0.0)
        nc.scalar.copy(out=early[:, 1:2], in_=early[:, 0:1])
        nc.sync.dma_start(offs_sb[:], offs)
        nc.sync.dma_start(out=xw_all[:], in_=x_words[0].rearrange("p n t -> p (n t)").bitcast(I32))
        w1_raw = [keep.tile([P, 2, H], F32, name=f"w1_raw{g}", align_bytes=64) for g in range(2)]
        for g in range(2):
            nc.sync.dma_start(out=w1_raw[g][:], in_=rows(w1)[:, 2 * g : 2 * g + 2, :])
        nc.sync.dma_start(p1_sb[:], p1)
        nc.sync.dma_start(p2_sb[:], p2)
        nc.vector.tensor_copy(xs_apart[:], xs_all[:].indirect(offs_sb[:]))
        for r in range(4):
            nc.scalar.dma_start(out=xs[r:P:32, :].bitcast(I32), in_=xs_apart[112 + r : P : 4, :].bitcast(I32))
        w2_raw = [placed(f"w2_raw{g}", [P, PACK, HALF], F32, 2.5 + 4 * g)[:] for g in range(2)]
        for g in range(2):
            nc.sync.dma_start(out=w2_raw[g], in_=rows(w2)[:, :, g * HALF : (g + 1) * HALF])
        w3_row = placed("w3_row", [P, 2 * H - SUB + PACK * W3_SPLIT], F32, 10.5)
        w_raw = {"w3": w3_row[:, 2 * H - SUB :].rearrange("p (j c) -> p j c", j=PACK)}
        nc.sync.dma_start(out=w_raw["w3"], in_=rows(w3)[:, :, 0:W3_SPLIT])

        ident = keep.tile([P, P], F32, name="ident")
        make_identity(nc, ident[:])
        names = ("w1", "w2", "w3", "w4")
        w_bf = {n: keep.tile([P, PACK * H], BF16, name=f"{n}_bf", align_bytes=64) for n in ("w4",)}
        w_bf["w3"] = w3_row[:, 0 : 2 * H].bitcast(BF16)
        w_bf["w1"] = placed("w1_bf", [P, PACK * H], BF16, 44)
        w_codes = {n: keep.tile([P, H], U32, name=f"{n}_codes", align_bytes=64) for n in ("w1", "w2")}
        w_scale = {n: keep.tile([P, H], U8, name=f"{n}_scale", align_bytes=64) for n in names}

        def cast_tile(copy, t, m0, m1):
            copy(out=w_bf["w1"][:, t * H : (t + 1) * H].rearrange("p (m j) -> p m j", j=PACK)[:, m0:m1, 2:4],
                 in_=w1_raw[1][:].rearrange("p j (m t) -> p t m j", t=PACK)[:, t, m0:m1])

        def cast_dealt(copy, n, raw, h, m0=0, m1=P):
            half = w_bf[n][:, h * 2 * H : (h + 1) * 2 * H]
            copy(out=half.rearrange("p (e m j) -> p m j e", e=2, j=PACK)[:, m0:m1, 2:4],
                 in_=raw[:].rearrange("p j (m h e) -> p h m j e", h=2, e=2)[:, h, m0:m1])

        def quantize_w(n):
            nc.vector.quantize_mx(out=w_codes[n][:].bitcast(FP8X4), scales=w_scale[n][:], in_=w_bf[n][:])

        def mm(dst, n, tile_index, codes, scales, start, stop):
            cols = slice(tile_index * P, (tile_index + 1) * P)
            nc.tensor.matmul_mx(out=dst, lhsT=w_codes[n][:, cols].bitcast(FP8X4), lhsT_scale=w_scale[n][:, cols],
                                rhs=codes.bitcast(FP8X4), rhs_scale=scales, start=start, stop=stop)

        nc.vector.tensor_copy(xw[:], xw_all[:].bitcast(U32).indirect(offs_sb[:]))

        def quantize_w1(c0, c1):
            nc.vector.quantize_mx(out=w_codes["w1"][:, c0:c1].bitcast(FP8X4), scales=w_scale["w1"][:, c0:c1], in_=w_bf["w1"][:, PACK * c0 : PACK * c1])

        for copy, m0, m1 in ((nc.vector.tensor_copy, 0, EARLY_SHARE), (nc.scalar.copy, EARLY_SHARE, P)):
            copy(out=w_bf["w1"][:].rearrange("p (t m j) -> p m j t", t=PACK, j=PACK)[:, m0:m1, 0:2], in_=w1_raw[0][:].rearrange("p j (m t) -> p m j t", t=PACK)[:, m0:m1])
        for t in range(2):
            cast_tile(nc.vector.tensor_copy, t, 0, SHARE)
            cast_tile(nc.scalar.copy, t, SHARE, P)
        quantize_w1(0, P)
        quantize_w1(P, 2 * P)
        cast_dealt(nc.scalar.copy, "w1", w1_raw[1], 1)
        quantize_w1(2 * P, 4 * P)

        w3_rest = keep.tile([P, PACK, H - W3_SPLIT], F32, name="w1_raw1", align_bytes=64)
        nc.sync.dma_start(out=w3_rest[:], in_=rows(w3)[:, :, W3_SPLIT:H])
        w_raw["w4"] = placed("w4_raw", [P, PACK, H], F32, 44)
        nc.sync.dma_start(out=w_raw["w4"][:], in_=rows(w4))

        w_bf["w2"] = keep.tile([P, PACK * H], BF16, name="w2_bf", align_bytes=64)
        h1 = [keep.tile([P, S], F32, name=f"h1_{t}") for t in range(PACK)]

        def cast_w2(g):
            nc.vector.tensor_copy(out=w_bf["w2"][:].rearrange("p (t m j) -> p m j t", t=PACK, j=PACK)[:, g * P // 2 : (g + 1) * P // 2],
                                  in_=w2_raw[g].rearrange("p j (m t) -> p m j t", t=PACK))

        y_win = [keep.tile([P, WINDOW], F32, name=f"y_win{t}") for t in range(PACK)]
        pieces = [(0, 0, HALF), (0, HALF, SUB), (0, HALF + SUB, SUB)] + [(t, 0, S) for t in range(1, PACK)]
        for index, (t, j0, width) in enumerate(pieces):
            cols = slice(j0, j0 + width)
            acc = bank(index % Y_BANKS, [P, width])
            mm(acc[:], "w1", t, xw[:, cols], xs[:, cols], True, True)
            copy = nc.vector.tensor_copy if index == 0 or t == 1 else nc.scalar.copy
            copy(out=y_win[t][:, cols], in_=acc[:])
            if t == 1:
                cast_w2(0)
            if j0 + width == S:
                nc.scalar.activation(h1[t][:], y_win[t][:].indirect(p1_sb[:]), COPY)

        def cast_in_place(copy, n, c0, c1, raw):
            copy(out=w_bf[n][:, PACK * c0 : PACK * c1].rearrange("p (c i j) -> p c j i", i=4, j=PACK),
                 in_=raw[:, :, c0:c1].rearrange("p j (c i) -> p c j i", i=4))

        cast_in_place(nc.scalar.copy, "w4", 0, H, w_raw["w4"])

        turned = [[bank(TURN_BANKS[h][b], [P, 2, 2, SUB]) for b in range(2)] for h in range(2)]

        def turn(src, t, first):
            for v in range(RUNS):
                edge = v % 2 == t % 2
                nc.tensor.matmul(turned[t // 2][v // 2][:, v % 2, t % 2, :], lhsT=src[:, v * SUB : (v + 1) * SUB], rhs=ident[:], is_transpose=True,
                                 start=first and edge and t % 2 == 0, stop=not first and edge and t % 2 == 1)

        for t in range(PACK):
            turn(y_win[t], t, True)

        def make_c(v):
            cols = slice(v * SUB, (v + 1) * SUB)
            own = bank(C_BANKS[v], [P, PACK, SUB])
            for t in range(PACK):
                mm(own[:, t, :], "w2", t, xw[:, cols], xs[:, cols], True, True)
            return own

        hs_row = keep.tile([P, PACK * S], F32, name="hs_row")
        hs = hs_row[:].rearrange("p (t s) -> p t s", t=PACK)
        for t in range(PACK):
            if t == 1:
                cast_w2(1)
            if t == 2:
                quantize_w("w2")
                c = {v: make_c(v) for v in range(2)}
            nc.vector.tensor_tensor(hs[:, t, :], y_win[t][:].indirect(p2_sb[:]), h1[t][:], ADD)
            turn(hs[:, t, :], t, False)
        cast_in_place(nc.vector.tensor_copy, "w3", 0, W3_SPLIT, w_raw["w3"])
        nc.gpsimd.tensor_copy(out=w_bf["w3"][:, PACK * W3_SPLIT : PACK * H].rearrange("p (c j) -> p c j", j=PACK),
                              in_=w3_rest[:].rearrange("p j c -> p c j"))

        wide = HALF * PACK
        z2_first = w3_row[:, 2 * H : 2 * H + wide // 2].bitcast(BF16)
        z_in = [placed(f"z_in{b}", [P, wide], BF16, 34 + 2 * b)[:] for b in range(2)]
        out_rows = out.rearrange("(a p) j -> p a j", p=P)

        def product(v, dst):
            cols = slice(v * SUB, (v + 1) * SUB)
            own = c[v]
            nc.vector.tensor_tensor(
                dst.rearrange("p (c i t) -> p c t i", i=2, t=PACK),
                own[:].rearrange("p t (c i) -> p c t i", i=2),
                hs[:, :, cols].rearrange("p t (c i) -> p c t i", i=2),
                MULT,
            )

        back = {}

        def turn_back(h, b):
            if h == 0:
                back[b] = bank(BACK_BANKS[b], [P, 2, 2, SUB])
            zt_bf = placed(f"zt{h}{b}", [P, 4 * SUB], BF16, (44, 45, 48, 51)[2 * h + b])[:]
            nc.scalar.copy(out=zt_bf.rearrange("k (u p e) -> k u p e", u=2, e=2), in_=turned[h][b][:].rearrange("k u e p -> k u p e"))
            if (h, b) == (0, 0):
                c[2] = make_c(2)
            for u in range(2):
                nc.tensor.transpose(back[b][:, u, h, :], zt_bf.bitcast(F32)[:, u * P : (u + 1) * P], ident[:])
            if (h, b) == (0, 1):
                c[3] = make_c(3)
            if h == 1:
                width = (S, HALF)[b]
                mm(bank(TURN_BANKS[h][b], [P, width])[:], "w2", 0, xw[:, 0:width], xs[:, 0:width], True, True)
                nc.scalar.copy(out=z_in[b].bitcast(F32).rearrange("p (u k h) -> p u k h", u=2, h=2), in_=back[b][:].rearrange("p u h k -> p u k h"))

        def quantize_z(name, src, kib):
            width = src.shape[1] // PACK
            codes = placed(f"{name}_codes", [P, width], U32, kib)
            scale = keep.tile([P, width], U8, name=f"{name}_scale", align_bytes=64)
            nc.vector.quantize_mx(out=codes[:].bitcast(FP8X4), scales=scale[:], in_=src)
            return codes, scale

        res = keep.tile([P, PACK, S], F32, name="res")
        product(0, z2_first[:, 0 : SUB * PACK])
        product(1, z2_first[:, SUB * PACK : wide])
        turn_back(0, 0)
        z2_third = w3_row[:, 2 * H + wide // 2 : 2 * H + 3 * wide // 4].bitcast(BF16)
        product(2, z2_third)
        w_codes["w4"] = placed("w4_codes", [P, H], U32, 42.5)
        quantize_w("w4")
        turn_back(0, 1)
        turn_back(1, 0)
        turn_back(1, 1)
        z2c, z2s = quantize_z("early", z2_first, 47.5)
        accs = [bank(index, [P, HALF]) for index in OUT_BANKS[0]]
        for a in range(PACK):
            mm(accs[a][:], "w4", a, z2c[:], z2s[:], True, False)
        w_codes["w3"] = placed("w3_codes", [P, H], U32, 48.5)
        quantize_w("w3")
        codes, scale = quantize_z("first", z_in[0], 30)
        for a in range(PACK):
            acc = accs[a]
            mm(acc[:], "w3", a, codes[:], scale[:], False, True)
            nc.scalar.copy(out=res[:, a, 0:HALF], in_=acc[:])
            nc.sync.dma_start(out=out_rows[:, a, 0:HALF], in_=res[:, a, 0:HALF])
        zc, zs = quantize_z("second", z_in[1], 31)
        z2c, z2s = quantize_z("third", z2_third, 34.5)
        third = slice(HALF, HALF + SUB)
        for g in range(2):
            acc = bank(OUT_BANKS[1][g], [P, 2, SUB])
            for a in range(2):
                mm(acc[:, a, :], "w3", 2 * g + a, zc[:, 0:SUB], zs[:, 0:SUB], True, False)
                mm(acc[:, a, :], "w4", 2 * g + a, z2c[:], z2s[:], False, True)
            copy = nc.scalar.copy if g == 0 else nc.vector.tensor_copy
            copy(out=res[:, 2 * g : 2 * g + 2, third], in_=acc[:])
            nc.sync.dma_start(out=out_rows[:, 2 * g : 2 * g + 2, third], in_=res[:, 2 * g : 2 * g + 2, third])
        z2_last = placed("z2_last", [P, SUB * PACK], BF16, 35)
        product(3, z2_last[:])
        accs = [bank(index, [P, SUB]) for index in OUT_BANKS[2]]
        for a in range(PACK):
            mm(accs[a][:], "w3", a, zc[:, SUB:HALF], zs[:, SUB:HALF], True, False)
        z2c, z2s = quantize_z("last", z2_last[:], 33)
        last = slice(HALF + SUB, S)
        for a in range(PACK):
            mm(accs[a][:], "w4", a, z2c[:], z2s[:], False, True)
        for a in range(PACK):
            copy = nc.scalar.copy if a % 2 == 1 else nc.vector.tensor_copy
            copy(out=res[:, a, last], in_=accs[a][:])
        nc.sync.dma_start(out=out_rows[:, 0:2, last], in_=res[:, 0:2, last])
        nc.scalar.dma_start(out=out_rows[:, 2:4, last], in_=res[:, 2:4, last])
